import numpy as np
import ml_dtypes


def mxq(x, axis, fmt="e4m3"):
    dtype, down = {"e4m3": (ml_dtypes.float8_e4m3fn, 7), "e5m2": (ml_dtypes.float8_e5m2, 14)}[fmt]
    v = np.moveaxis(np.asarray(x, np.float32).astype(ml_dtypes.bfloat16).astype(np.float64), axis, -1)
    blocks = v.reshape(v.shape[:-1] + (-1, 32))
    amax = np.abs(blocks).max(-1, keepdims=True)
    byte = np.maximum(np.where(amax > 0, np.frexp(amax)[1] - 1 + 127, 0) - down, 1)
    scale = np.exp2(byte - 127.0)
    codes = (blocks / scale).astype(np.float32).astype(dtype).astype(np.float64)
    return np.moveaxis((codes * scale).reshape(v.shape), -1, axis)


WIDE = False


def mx_kscale(k):
    if not WIDE:
        return np.ones(k)
    levels = np.array([10, -10, 5, -5, 0])
    if k % 512:
        return np.exp2(np.random.permutation(np.resize(levels, k // 32))).repeat(32)
    a = np.empty((k // 512, 16))
    for p in range(k // 512):
        a[p, :8] = np.random.permutation(np.resize(levels, 8))
        for g in range(8):
            far = levels[np.abs(levels - a[p, g]) >= 10]
            a[p, g + 8] = far[np.random.randint(len(far))]
    return np.exp2(a.ravel()).repeat(32)


BF16 = ml_dtypes.bfloat16


def bf(x):
    return np.asarray(x, np.float32).astype(BF16)


def f64(x):
    return np.asarray(x).astype(np.float64)


E2M1 = np.array([0.0, 0.5, 1.0, 1.5, 2.0, 3.0, 4.0, 6.0, -0.0, -0.5, -1.0, -1.5, -2.0, -3.0, -4.0, -6.0])


def pack_weight(w, fmt):
    k, n = w.shape
    w = f64(bf(w)).reshape(k // 32, 32, n)
    amax = np.abs(w).max(1)
    if fmt == "e4m3":
        byte = np.frexp(amax)[1] - 1 + 127 - 7
    else:
        mant, ex = np.frexp(amax / 6.0)
        byte = np.where(mant > 0.5, ex, ex - 1) + 127
    byte = np.clip(np.where(amax > 0, byte, 1), 1, 254)
    scaled = (w * np.exp2(127.0 - byte)[:, None, :]).reshape(k, n).astype(np.float32)
    by_word = np.ascontiguousarray(scaled.reshape(k // 512, 128, 4, n).transpose(0, 1, 3, 2))
    if fmt == "e4m3":
        words = by_word.astype(ml_dtypes.float8_e4m3fn).view(np.uint8)
    else:
        c = by_word.astype(ml_dtypes.float4_e2m1fn).view(np.uint8) & 0xF
        words = c[..., 0::2] | (c[..., 1::2] << 4)
    return np.ascontiguousarray(words), np.ascontiguousarray(byte.astype(np.uint8).reshape(k // 512, 16, n))


def unpack_weight(words, scales, fmt):
    g, p, n, _ = words.shape
    if fmt == "e4m3":
        vals = np.ascontiguousarray(words).view(ml_dtypes.float8_e4m3fn).astype(np.float64)
    else:
        nib = np.empty((g, p, n, 4), np.uint8)
        nib[..., 0::2] = words & 0xF
        nib[..., 1::2] = words >> 4
        vals = E2M1[nib]
    vals = vals * np.repeat(np.exp2(scales.astype(np.float64) - 127.0), 8, axis=1)[..., None]
    return vals.transpose(0, 1, 3, 2).reshape(g * 512, n)
def pack4(w):
    words, scales = pack_weight(w, "e2m1")
    return words.reshape(words.shape[0], 128, -1), scales


def unpack4(words, scales):
    return unpack_weight(words.reshape(words.shape[0], 128, -1, 2), scales, "e2m1")


M, D, N, E = 1024, 1024, 2048, 1024

EPS = 0.8
TAU = 0.75


def setup_inputs():
    s, t = mx_kscale(D), mx_kscale(N)
    cloud = np.random.standard_normal((M, D)) + 0.5 * np.random.standard_normal(D)
    y_words, y_scales = pack4(np.random.standard_normal((D, N)) / np.sqrt(D) / s[:, None])
    z_words, z_scales = pack4(np.random.standard_normal((N, E)) / np.sqrt(N) / t[:, None])
    return {"x": bf(cloud * s),
            "y_words": y_words,
            "y_scales": y_scales,
            "a": bf(np.exp(0.8 * np.random.standard_normal(M))),
            "b": bf(np.exp(0.4 * np.random.standard_normal(N))),
            "gain": bf((1 + 0.1 * np.random.standard_normal(N)) * t),
            "z_words": z_words,
            "z_scales": z_scales,
            "start": bf(np.random.standard_normal((M, E)))}


def reference(x, y_words, y_scales, a, b, gain, z_words, z_scales, start):
    sim = mxq(f64(x), 1, "e4m3") @ unpack4(y_words, y_scales)
    kern = np.exp((sim - sim.max(axis=1, keepdims=True)) / EPS)
    u = f64(a)[:, None] / kern.mean(axis=1, keepdims=True)
    rows = u * kern
    v = f64(b)[None, :] / rows.mean(axis=0, keepdims=True)
    plan = rows * v
    mass = plan.mean(axis=1, keepdims=True)
    weighted = plan * f64(gain)[None, :]
    bary = (mxq(weighted, 1, "e4m3") @ unpack4(z_words, z_scales)) / mass
    return (1 - TAU) * f64(start) + TAU * bary

@@ -1,0 +1,244 @@
+from contextlib import ExitStack
+
+import concourse.mybir as mybir
+from concourse.masks import make_identity
+
+M, D, N, E = 1024, 1024, 2048, 1024
+FLOPS = 2 * M * D * N + 2 * M * N * E
+
+F32 = mybir.dt.float32
+BF16 = mybir.dt.bfloat16
+I32 = mybir.dt.int32
+U32 = mybir.dt.uint32
+U8 = mybir.dt.uint8
+FP8X4 = mybir.dt.float8_e4m3fn_x4
+FP4X4 = mybir.dt.float4_e2m1fn_x4
+ADD = mybir.AluOpType.add
+MULT = mybir.AluOpType.mult
+MIN = mybir.AluOpType.min
+AX = mybir.AxisListType.X
+ACT = mybir.ActivationFunctionType
+
+P = 128
+KP = 512
+MT = M // P
+GD = D // KP
+GN = N // KP
+NP = 4
+W = 256
+
+
+def tile_sinkhorn_step_barycentre_f1_kernel(tc, x, y_words, y_scales, a, b, gain, z_words, z_scales, start, out):
+    nc = tc.nc
+    with ExitStack() as ctx:
+        keep = ctx.enter_context(tc.tile_pool(name="keep", bufs=1))
+        work = ctx.enter_context(tc.tile_pool(name="work", bufs=3))
+        psum = ctx.enter_context(tc.psum_pool(name="psum", bufs=4))
+
+        ident = keep.tile([P, P], F32, name="ident")
+        make_identity(nc, ident[:])
+        warm = keep.tile([P, 1], F32, name="warm")
+        nc.vector.memset(warm[:], 0.0)
+        nc.scalar.activation(warm[:], warm[:], ACT.Exp)
+
+        y_plane = keep.tile([P, GD, N], U8, name="y_plane", align_bytes=64)
+        z_plane = keep.tile([P, GN, E], U8, name="z_plane", align_bytes=64)
+        nc.vector.memset(y_plane[:].rearrange("p g n -> p (g n)").bitcast(I32), 0)
+        nc.vector.memset(z_plane[:].rearrange("p g n -> p (g n)").bitcast(I32), 0)
+
+        x_view = x.rearrange("(p i) d -> p i d", i=MT)
+        start_view = start.rearrange("(p i) e -> p i e", i=MT)
+        out_view = out.rearrange("(p i) e -> p i e", i=MT)
+
+        xs = [keep.tile([P, D], BF16, name="x%d" % i, align_bytes=64) for i in range(MT)]
+        ys = [keep.tile([P, GD, 2 * KP], U8, name="y%d" % c, align_bytes=64) for c in range(GN)]
+        zs = keep.tile([P, GN, 2 * E], U8, name="zs", align_bytes=64)
+        st = [keep.tile([P, E], BF16, name="st%d" % i) for i in range(MT)]
+        a_sb = keep.tile([P, MT], BF16, name="a_sb")
+        b_sb = keep.tile([P, GN, 4], BF16, name="b_sb")
+        gain_sb = keep.tile([P, GN, 4], BF16, name="gain_sb")
+
+        def load_x(i):
+            nc.sync.dma_start(out=xs[i][:], in_=x_view[:, i, :])
+
+        def load_y(c):
+            nc.sync.dma_start(
+                out=ys[c][:].bitcast(I32),
+                in_=y_words[:, :, 2 * KP * c:2 * KP * (c + 1)].rearrange("g p n -> p g n").bitcast(I32),
+            )
+
+        def load_scales(plane, scales):
+            for q in range(4):
+                nc.sync.dma_start(
+                    out=plane[32 * q:32 * q + 4, :, :].bitcast(I32),
+                    in_=scales[:, 4 * q:4 * q + 4, :].rearrange("g r n -> r g n").bitcast(I32),
+                )
+
+        load_x(0)
+        load_y(0)
+        load_scales(y_plane, y_scales)
+        load_x(1)
+        load_y(1)
+        load_y(2)
+        load_y(3)
+        load_x(2)
+        nc.sync.dma_start(out=a_sb[:], in_=a.rearrange("(p i) -> p i", i=MT))
+        for i in range(3, MT):
+            load_x(i)
+        nc.sync.dma_start(out=b_sb[:], in_=b.rearrange("(g p t) -> p g t", p=P, t=4))
+        nc.sync.dma_start(out=gain_sb[:], in_=gain.rearrange("(g p t) -> p g t", p=P, t=4))
+        load_scales(z_plane, z_scales)
+        nc.sync.dma_start(out=zs[:].bitcast(I32), in_=z_words.rearrange("g p n -> p g n").bitcast(I32))
+        for i in range(MT):
+            nc.sync.dma_start(out=st[i][:], in_=start_view[:, i, :])
+
+        a_n = keep.tile([P, MT], F32, name="a_n")
+        nc.vector.tensor_scalar(a_n[:], a_sb[:], float(N), None, MULT)
+
+        x_codes = {}
+        x_planes = {}
+
+        def x_prep(i):
+            words = xs[i][:].bitcast(F32)
+            xt = psum.tile([P, GD, 2, P], F32, name="xt", tag="t")
+            for g in range(GD):
+                for u in range(2):
+                    nc.tensor.transpose(xt[:, g, u, :], words[:, 256 * g + u:256 * (g + 1):2], ident[:])
+            xg = work.tile([P, GD, P, 4], BF16, name="xg", align_bytes=64)
+            dst = xg[:].rearrange("p g r t -> p g (r t)").bitcast(F32).rearrange("p g (r u) -> p g r u", u=2)
+            nc.scalar.copy(dst, xt[:].rearrange("p g u r -> p g r u"))
+            codes = keep.tile([P, GD, P], U32, name="x_codes%d" % i, align_bytes=64)
+            plane = keep.tile([P, GD, P], U8, name="x_plane%d" % i, align_bytes=64)
+            nc.vector.quantize_mx(
+                out=codes[:].rearrange("p g r -> p (g r)").bitcast(FP8X4),
+                scales=plane[:].rearrange("p g r -> p (g r)"),
+                in_=xg[:].rearrange("p g r t -> p (g r t)"),
+            )
+            x_codes[i] = codes
+            x_planes[i] = plane
+
+        kern = {}
+        shift = {}
+        rsum = {}
+
+        def stage1(i):
+            z = work.tile([P, GN, 4, P], F32, name="kern", tag="kern", bufs=5)
+            mins = work.tile([P, GN], F32, name="mins", tag="mins")
+            for c in range(GN):
+                ps = psum.tile([P, KP], F32, name="ps", tag="s")
+                for g in range(GD):
+                    nc.tensor.matmul_mx(
+                        out=ps[:],
+                        lhsT=x_codes[i][:, g, :].bitcast(FP8X4),
+                        lhsT_scale=x_planes[i][:, g, :],
+                        rhs=ys[c][:, g, :].bitcast(FP4X4),
+                        rhs_scale=y_plane[:, g, KP * c:KP * (c + 1)],
+                        start=(g == 0),
+                        stop=(g == GD - 1),
+                    )
+                nc.vector.tensor_scalar(
+                    z[:, c, :, :], ps[:].rearrange("m (p t) -> m t p", t=4), -1.25, None, MULT, MIN, accum_out=mins[:, c:c + 1]
+                )
+            sh = work.tile([P, 1], F32, name="sh", tag="sh")
+            nc.vector.tensor_reduce(sh[:], mins[:], AX, MIN)
+            kern[i] = z
+            shift[i] = sh
+
+        def expo(i):
+            rs = work.tile([P, 1], F32, name="rs", tag="rs")
+            nc.scalar.activation(kern[i][:], kern[i][:], ACT.Exp, bias=shift[i][:], scale=-1.0, accum_out=rs[:])
+            rec = work.tile([P, 1], F32, name="rec", tag="rec")
+            nc.vector.reciprocal(rec[:], rs[:])
+            nc.gpsimd.tensor_scalar(kern[i][:], kern[i][:], rec[:], a_n[:, i:i + 1], MULT, MULT)
+
+        rt = {}
+        csum = keep.tile([P, GN, 4, NP], F32, name="csum")
+
+        def turn(k, half):
+            for g in (2 * half, 2 * half + 1):
+                r = keep.tile([P, 4, W], F32, name="rt%d_%d" % (k, g))
+                rt[k, g] = r
+                for tt in range(2):
+                    bank = psum.tile([P, 2, 2, P], F32, name="bank", tag="t")
+                    for t in range(2):
+                        for s in range(2):
+                            nc.tensor.transpose(bank[:, t, s, :], kern[2 * k + s][:, g, 2 * tt + t, :], ident[:])
+                    for t in range(2):
+                        j = 2 * tt + t
+                        acc = csum[:, g, j, k:k + 1]
+                        src = bank[:, t, :, :].rearrange("p s m -> p (s m)")
+                        if tt == 0:
+                            nc.vector.tensor_scalar(r[:, j, :], src, 1.0, None, MULT, ADD, accum_out=acc)
+                        else:
+                            nc.scalar.activation(r[:, j, :], src, ACT.Copy, accum_out=acc)
+
+        x_prep(0)
+        x_prep(1)
+        for i in range(MT + 3):
+            if i + 2 < MT:
+                x_prep(i + 2)
+            if i < MT:
+                stage1(i)
+            if 1 <= i <= MT:
+                expo(i - 1)
+            if i >= 3:
+                turn((i - 3) // 2, (i - 3) % 2)
+
+        v = keep.tile([P, GN, 4], F32, name="v")
+        vg = keep.tile([P, GN, 4], F32, name="vg")
+        vm = keep.tile([P, GN, 4], F32, name="vm")
+        tot = keep.tile([P, GN, 4], F32, name="tot")
+        rtot = keep.tile([P, GN, 4], F32, name="rtot")
+        for g in range(GN):
+            nc.vector.tensor_reduce(tot[:, g, :], csum[:, g, :, :], AX, ADD)
+            nc.vector.reciprocal(rtot[:, g, :], tot[:, g, :])
+            nc.vector.scalar_tensor_tensor(v[:, g, :], rtot[:, g, :], float(M), b_sb[:, g, :], MULT, MULT)
+            nc.vector.tensor_tensor(vg[:, g, :], v[:, g, :], gain_sb[:, g, :], MULT)
+            nc.vector.tensor_scalar(vm[:, g, :], v[:, g, :], 1.0 / (0.75 * N), None, MULT)
+
+        sq = []
+        for i in range(MT):
+            q = keep.tile([P, E], BF16, name="sq%d" % i)
+            nc.gpsimd.tensor_scalar(q[:], st[i][:], 0.25, 0.0, MULT, ADD)
+            sq.append(q)
+
+        for k in range(NP):
+            codes = []
+            planes = []
+            for g in range(GN):
+                gb = work.tile([P, 4, W], BF16, name="gb", tag="gb")
+                for t in range(4):
+                    nc.scalar.activation(gb[:, t, :], rt[k, g][:, t, :], ACT.Copy, scale=vg[:, g, t:t + 1])
+                gi = work.tile([P, W, 4], BF16, name="gi", tag="gi", align_bytes=64)
+                nc.vector.tensor_copy(gi[:], gb[:].rearrange("p t m -> p m t"))
+                cd = work.tile([P, W], U32, name="cd", tag="cd", bufs=8, align_bytes=64)
+                pl = work.tile([P, W], U8, name="pl", tag="pl", bufs=8, align_bytes=64)
+                nc.vector.quantize_mx(out=cd[:].bitcast(FP8X4), scales=pl[:], in_=gi[:].rearrange("p m t -> p (m t)"))
+                codes.append(cd)
+                planes.append(pl)
+            for s in range(2):
+                i = 2 * k + s
+                cols = slice(P * s, P * (s + 1))
+                mp = psum.tile([P, 1], F32, name="mp", tag="t")
+                for j in range(16):
+                    nc.tensor.matmul(
+                        mp[:], lhsT=rt[k, j // 4][:, j % 4, cols], rhs=vm[:, j // 4, j % 4:j % 4 + 1], start=(j == 0), stop=(j == 15)
+                    )
+                inv = work.tile([P, 1], F32, name="inv", tag="inv")
+                nc.vector.reciprocal(inv[:], mp[:])
+                for e in range(2):
+                    ecols = slice(KP * e, KP * (e + 1))
+                    ps = psum.tile([P, KP], F32, name="ps", tag="s")
+                    for g in range(GN):
+                        nc.tensor.matmul_mx(
+                            out=ps[:],
+                            lhsT=codes[g][:, cols].bitcast(FP8X4),
+                            lhsT_scale=planes[g][:, cols],
+                            rhs=zs[:, g, 2 * KP * e:2 * KP * (e + 1)].bitcast(FP4X4),
+                            rhs_scale=z_plane[:, g, ecols],
+                            start=(g == 0),
+                            stop=(g == GN - 1),
+                        )
+                    res = work.tile([P, KP], F32, name="res", tag="res", bufs=4)
+                    nc.vector.scalar_tensor_tensor(res[:], ps[:], inv[:], sq[i][:, ecols], MULT, ADD)
+                    nc.sync.dma_start(out=out_view[:, i, ecols], in_=res[:])

@@ -26,6 +26,7 @@ GD = D // KP
 GN = N // KP
 NP = 4
 W = 256
+G_ORDER = (0, 1, 2, 3)
 
 
 def tile_sinkhorn_step_barycentre_f1_kernel(tc, x, y_words, y_scales, a, b, gain, z_words, z_scales, start, out):
@@ -34,17 +35,19 @@ def tile_sinkhorn_step_barycentre_f1_kernel(tc, x, y_words, y_scales, a, b, gain
         keep = ctx.enter_context(tc.tile_pool(name="keep", bufs=1))
         work = ctx.enter_context(tc.tile_pool(name="work", bufs=3))
         psum = ctx.enter_context(tc.psum_pool(name="psum", bufs=4))
-
-        ident = keep.tile([P, P], F32, name="ident")
-        make_identity(nc, ident[:])
-        warm = keep.tile([P, 1], F32, name="warm")
-        nc.vector.memset(warm[:], 0.0)
-        nc.scalar.activation(warm[:], warm[:], ACT.Exp)
+        ctx.enter_context(tc.manual_schedule())
 
         y_plane = keep.tile([P, GD, N], U8, name="y_plane", align_bytes=64)
         z_plane = keep.tile([P, GN, E], U8, name="z_plane", align_bytes=64)
+        warm = keep.tile([P, 1], F32, name="warm")
+        ones = keep.tile([P, 1], F32, name="ones")
+        ident = keep.tile([P, P], F32, name="ident")
         nc.vector.memset(y_plane[:].rearrange("p g n -> p (g n)").bitcast(I32), 0)
+        nc.vector.memset(warm[:], 0.0)
+        nc.vector.memset(ones[:], 1.0)
         nc.vector.memset(z_plane[:].rearrange("p g n -> p (g n)").bitcast(I32), 0)
+        make_identity(nc, ident[:])
+        nc.scalar.activation(warm[:], warm[:], ACT.Exp)
 
         x_view = x.rearrange("(p i) d -> p i d", i=MT)
         start_view = start.rearrange("(p i) e -> p i e", i=MT)
@@ -75,10 +78,10 @@ def tile_sinkhorn_step_barycentre_f1_kernel(tc, x, y_words, y_scales, a, b, gain
                 )
 
         load_x(0)
-        load_y(0)
         load_scales(y_plane, y_scales)
-        load_x(1)
+        load_y(0)
         load_y(1)
+        load_x(1)
         load_y(2)
         load_y(3)
         load_x(2)
@@ -93,152 +96,367 @@ def tile_sinkhorn_step_barycentre_f1_kernel(tc, x, y_words, y_scales, a, b, gain
             nc.sync.dma_start(out=st[i][:], in_=start_view[:, i, :])
 
         a_n = keep.tile([P, MT], F32, name="a_n")
-        nc.vector.tensor_scalar(a_n[:], a_sb[:], float(N), None, MULT)
-
         x_codes = {}
         x_planes = {}
+        x_words = {}
 
-        def x_prep(i):
+        def x_turn(i):
             words = xs[i][:].bitcast(F32)
             xt = psum.tile([P, GD, 2, P], F32, name="xt", tag="t")
             for g in range(GD):
                 for u in range(2):
                     nc.tensor.transpose(xt[:, g, u, :], words[:, 256 * g + u:256 * (g + 1):2], ident[:])
+            x_words[i] = xt
+
+        def x_copy(i):
             xg = work.tile([P, GD, P, 4], BF16, name="xg", align_bytes=64)
             dst = xg[:].rearrange("p g r t -> p g (r t)").bitcast(F32).rearrange("p g (r u) -> p g r u", u=2)
-            nc.scalar.copy(dst, xt[:].rearrange("p g u r -> p g r u"))
+            nc.scalar.copy(dst, x_words[i][:].rearrange("p g u r -> p g r u"))
+            x_words[i] = xg
+
+        def x_quant(i):
             codes = keep.tile([P, GD, P], U32, name="x_codes%d" % i, align_bytes=64)
             plane = keep.tile([P, GD, P], U8, name="x_plane%d" % i, align_bytes=64)
             nc.vector.quantize_mx(
                 out=codes[:].rearrange("p g r -> p (g r)").bitcast(FP8X4),
                 scales=plane[:].rearrange("p g r -> p (g r)"),
-                in_=xg[:].rearrange("p g r t -> p (g r t)"),
+                in_=x_words[i][:].rearrange("p g r t -> p (g r t)"),
             )
             x_codes[i] = codes
             x_planes[i] = plane
 
         kern = {}
+        mins = {}
         shift = {}
-        rsum = {}
+        banks = {}
 
-        def stage1(i):
-            z = work.tile([P, GN, 4, P], F32, name="kern", tag="kern", bufs=5)
-            mins = work.tile([P, GN], F32, name="mins", tag="mins")
-            for c in range(GN):
-                ps = psum.tile([P, KP], F32, name="ps", tag="s")
-                for g in range(GD):
-                    nc.tensor.matmul_mx(
-                        out=ps[:],
-                        lhsT=x_codes[i][:, g, :].bitcast(FP8X4),
-                        lhsT_scale=x_planes[i][:, g, :],
-                        rhs=ys[c][:, g, :].bitcast(FP4X4),
-                        rhs_scale=y_plane[:, g, KP * c:KP * (c + 1)],
-                        start=(g == 0),
-                        stop=(g == GD - 1),
-                    )
-                nc.vector.tensor_scalar(
-                    z[:, c, :, :], ps[:].rearrange("m (p t) -> m t p", t=4), -1.25, None, MULT, MIN, accum_out=mins[:, c:c + 1]
+        def sim_mm(i, c):
+            ps = psum.tile([P, KP], F32, name="ps", tag="s")
+            for g in range(GD):
+                nc.tensor.matmul_mx(
+                    out=ps[:],
+                    lhsT=x_codes[i][:, g, :].bitcast(FP8X4),
+                    lhsT_scale=x_planes[i][:, g, :],
+                    rhs=ys[c][:, g, :].bitcast(FP4X4),
+                    rhs_scale=y_plane[:, g, KP * c:KP * (c + 1)],
+                    start=(g == 0),
+                    stop=(g == GD - 1),
                 )
+            banks[i, c] = ps
+
+        def sim_out(i, c):
+            if c == 0:
+                kern[i] = work.tile([P, GN, 4, P], F32, name="kern", tag="kern", bufs=5)
+                mins[i] = work.tile([P, GN], F32, name="mins", tag="mins")
+            nc.vector.tensor_scalar(
+                kern[i][:, c, :, :], banks[i, c][:].rearrange("m (p t) -> m t p", t=4), -1.25, None, MULT, MIN, accum_out=mins[i][:, c:c + 1]
+            )
+
+        def row_min(i):
             sh = work.tile([P, 1], F32, name="sh", tag="sh")
-            nc.vector.tensor_reduce(sh[:], mins[:], AX, MIN)
-            kern[i] = z
+            nc.vector.tensor_reduce(sh[:], mins[i][:], AX, MIN)
             shift[i] = sh
+
+        rsum = {}
 
         def expo(i):
             rs = work.tile([P, 1], F32, name="rs", tag="rs")
             nc.scalar.activation(kern[i][:], kern[i][:], ACT.Exp, bias=shift[i][:], scale=-1.0, accum_out=rs[:])
+            rsum[i] = rs
+
+        def row_scale(i):
             rec = work.tile([P, 1], F32, name="rec", tag="rec")
-            nc.vector.reciprocal(rec[:], rs[:])
-            nc.gpsimd.tensor_scalar(kern[i][:], kern[i][:], rec[:], a_n[:, i:i + 1], MULT, MULT)
+            nc.vector.reciprocal(rec[:], rsum[i][:])
+            if i < MT - 1:
+                nc.gpsimd.tensor_scalar(kern[i][:], kern[i][:], rec[:], a_n[:, i:i + 1], MULT, MULT)
+            else:
+                for g in range(GN):
+                    eng = nc.vector if g < 3 else nc.gpsimd
+                    eng.tensor_scalar(kern[i][:, g, :, :], kern[i][:, g, :, :], rec[:], a_n[:, i:i + 1], MULT, MULT)
+
+        def turn_outs(k, g, engs):
+            for j in range(4):
+                turn_out(k, g, j, engs[j])
 
         rt = {}
+        tb = {}
         csum = keep.tile([P, GN, 4, NP], F32, name="csum")
 
-        def turn(k, half):
-            for g in (2 * half, 2 * half + 1):
-                r = keep.tile([P, 4, W], F32, name="rt%d_%d" % (k, g))
-                rt[k, g] = r
-                for tt in range(2):
-                    bank = psum.tile([P, 2, 2, P], F32, name="bank", tag="t")
-                    for t in range(2):
-                        for s in range(2):
-                            nc.tensor.transpose(bank[:, t, s, :], kern[2 * k + s][:, g, 2 * tt + t, :], ident[:])
-                    for t in range(2):
-                        j = 2 * tt + t
-                        acc = csum[:, g, j, k:k + 1]
-                        src = bank[:, t, :, :].rearrange("p s m -> p (s m)")
-                        if tt == 0:
-                            nc.vector.tensor_scalar(r[:, j, :], src, 1.0, None, MULT, ADD, accum_out=acc)
-                        else:
-                            nc.scalar.activation(r[:, j, :], src, ACT.Copy, accum_out=acc)
+        def turn(k, g, tt):
+            bank = psum.tile([P, 2, 2, P], F32, name="bank", tag="t")
+            for t in range(2):
+                for s in range(2):
+                    nc.tensor.transpose(bank[:, t, s, :], kern[2 * k + s][:, g, 2 * tt + t, :], ident[:])
+            tb[k, g, tt] = bank
 
-        x_prep(0)
-        x_prep(1)
-        for i in range(MT + 3):
+        def turn_out(k, g, j, eng):
+            if (k, g) not in rt:
+                rt[k, g] = keep.tile([P, 4, W], F32, name="rt%d_%d" % (k, g))
+            acc = csum[:, g, j, k:k + 1]
+            src = tb[k, g, j // 2][:, j % 2, :, :].rearrange("p s m -> p (s m)")
+            if eng == "v":
+                nc.vector.tensor_scalar(rt[k, g][:, j, :], src, 1.0, None, MULT, ADD, accum_out=acc)
+            else:
+                nc.scalar.activation(rt[k, g][:, j, :], src, ACT.Copy, accum_out=acc)
+
+        sq = [keep.tile([P, E], BF16, name="sq%d" % i) for i in range(MT)]
+
+        def turn_outs(k, g, engs):
+            for j in range(4):
+                turn_out(k, g, j, engs[j])
+
+        x_turn(0)
+        x_copy(0)
+        x_quant(0)
+        for i in range(MT):
+            k, half = divmod(i - 3, 2)
+            gs = (2 * half, 2 * half + 1) if i >= 3 else ()
+            for c in range(GN):
+                sim_mm(i, c)
+                if i == 0 and c == 1:
+                    x_turn(1)
+                    x_copy(1)
             if i + 2 < MT:
-                x_prep(i + 2)
-            if i < MT:
-                stage1(i)
-            if 1 <= i <= MT:
-                expo(i - 1)
-            if i >= 3:
-                turn((i - 3) // 2, (i - 3) % 2)
+                x_turn(i + 2)
+            for g in gs:
+                turn(k, g, 0)
+                turn(k, g, 1)
+            for c in range(GN):
+                sim_out(i, c)
+                if i == 0 and c == 2:
+                    x_quant(1)
+            row_min(i)
+            if i == 0:
+                nc.vector.tensor_scalar(a_n[:], a_sb[:], float(N), None, MULT)
+            if i >= 1:
+                row_scale(i - 1)
+            if i >= 4:
+                nc.gpsimd.tensor_scalar(sq[i - 4][:], st[i - 4][:], 0.25, 0.0, MULT, ADD)
+            if i + 2 < MT:
+                x_copy(i + 2)
+            expo(i)
+            for g in gs:
+                turn_outs(k, g, "vsvs" if i + 1 < MT else "vvvv")
+            if i + 2 < MT:
+                x_quant(i + 2)
+        turn(2, 2, 0)
+        turn(2, 2, 1)
+        turn(2, 3, 0)
+        turn(2, 3, 1)
+        turn_outs(2, 2, "vssv")
+        row_scale(MT - 1)
+        turn_outs(2, 3, "ssvs")
 
         v = keep.tile([P, GN, 4], F32, name="v")
         vg = keep.tile([P, GN, 4], F32, name="vg")
         vm = keep.tile([P, GN, 4], F32, name="vm")
         tot = keep.tile([P, GN, 4], F32, name="tot")
         rtot = keep.tile([P, GN, 4], F32, name="rtot")
-        for g in range(GN):
-            nc.vector.tensor_reduce(tot[:, g, :], csum[:, g, :, :], AX, ADD)
-            nc.vector.reciprocal(rtot[:, g, :], tot[:, g, :])
-            nc.vector.scalar_tensor_tensor(v[:, g, :], rtot[:, g, :], float(M), b_sb[:, g, :], MULT, MULT)
-            nc.vector.tensor_tensor(vg[:, g, :], v[:, g, :], gain_sb[:, g, :], MULT)
-            nc.vector.tensor_scalar(vm[:, g, :], v[:, g, :], 1.0 / (0.75 * N), None, MULT)
 
-        sq = []
-        for i in range(MT):
-            q = keep.tile([P, E], BF16, name="sq%d" % i)
-            nc.gpsimd.tensor_scalar(q[:], st[i][:], 0.25, 0.0, MULT, ADD)
-            sq.append(q)
+        def col_scale(h):
+            gs = slice(2 * h, 2 * h + 2)
+            return [
+                lambda: nc.vector.tensor_reduce(tot[:, gs, :], csum[:, gs, :, :], AX, ADD),
+                lambda: nc.vector.reciprocal(rtot[:, gs, :], tot[:, gs, :]),
+                lambda: nc.vector.scalar_tensor_tensor(v[:, gs, :], rtot[:, gs, :], float(M), b_sb[:, gs, :], MULT, MULT),
+                lambda: nc.vector.tensor_tensor(vg[:, gs, :], v[:, gs, :], gain_sb[:, gs, :], MULT),
+                lambda: nc.vector.tensor_scalar(vm[:, gs, :], v[:, gs, :], 1.0 / (0.75 * N), None, MULT),
+            ]
 
-        for k in range(NP):
-            codes = []
-            planes = []
-            for g in range(GN):
-                gb = work.tile([P, 4, W], BF16, name="gb", tag="gb")
-                for t in range(4):
-                    nc.scalar.activation(gb[:, t, :], rt[k, g][:, t, :], ACT.Copy, scale=vg[:, g, t:t + 1])
-                gi = work.tile([P, W, 4], BF16, name="gi", tag="gi", align_bytes=64)
-                nc.vector.tensor_copy(gi[:], gb[:].rearrange("p t m -> p m t"))
-                cd = work.tile([P, W], U32, name="cd", tag="cd", bufs=8, align_bytes=64)
-                pl = work.tile([P, W], U8, name="pl", tag="pl", bufs=8, align_bytes=64)
-                nc.vector.quantize_mx(out=cd[:].bitcast(FP8X4), scales=pl[:], in_=gi[:].rearrange("p m t -> p (m t)"))
-                codes.append(cd)
-                planes.append(pl)
-            for s in range(2):
-                i = 2 * k + s
-                cols = slice(P * s, P * (s + 1))
-                mp = psum.tile([P, 1], F32, name="mp", tag="t")
-                for j in range(16):
+        for q in range(4, MT):
+            nc.gpsimd.tensor_scalar(sq[q][:], st[q][:], 0.25, 0.0, MULT, ADD)
+
+        gb = {}
+        gi = {}
+        codes = {}
+        planes = {}
+
+        def scale(k, g):
+            gb[k, g] = work.tile([P, 4, W], BF16, name="gb", tag="gb", bufs=5)
+            for t in range(4):
+                nc.scalar.activation(gb[k, g][:, t, :], rt[k, g][:, t, :], ACT.Copy, scale=vg[:, g, t:t + 1])
+
+        def interleave(k, g, eng):
+            gi[k, g] = work.tile([P, W, 4], BF16, name="gi", tag="gi", bufs=5, align_bytes=64)
+            dst = gi[k, g][:].rearrange("p (c i) t -> p c t i", i=4)
+            src = gb[k, g][:].rearrange("p t (c i) -> p c t i", i=4)
+            if eng == "s":
+                nc.scalar.copy(dst, src)
+            else:
+                nc.vector.tensor_copy(dst, src)
+
+        def quant(k, g):
+            codes[k, g] = work.tile([P, W], U32, name="cd", tag="cd", bufs=8, align_bytes=64)
+            planes[k, g] = work.tile([P, W], U8, name="pl", tag="pl", bufs=8, align_bytes=64)
+            nc.vector.quantize_mx(
+                out=codes[k, g][:].bitcast(FP8X4), scales=planes[k, g][:], in_=gi[k, g][:].rearrange("p m t -> p (m t)")
+            )
+
+        mass_acc = {}
+        mbank = {}
+        on_pe = {0: (3,), 1: (3,), 2: (3,), 3: (3,)}
+
+        def mass_v(k, g):
+            ops = []
+            for t in range(4):
+                if t in on_pe[k]:
+                    continue
+                src, scl = rt[k, g][:, t, :], vm[:, g, t:t + 1]
+                if k not in mass_acc:
+                    mass_acc[k] = work.tile([P, W], F32, name="macc", tag="macc", bufs=2)
+                    ops.append(lambda src=src, scl=scl: nc.vector.tensor_scalar(mass_acc[k][:], src, scl, None, MULT))
+                else:
+                    ops.append(lambda src=src, scl=scl: nc.vector.scalar_tensor_tensor(mass_acc[k][:], src, scl, mass_acc[k][:], MULT, ADD))
+            return ops
+
+        def mass_t(k, gs):
+            if k not in mbank:
+                mbank[k] = psum.tile([P, W], F32, name="mb", tag="t")
+            for g in gs:
+                for t in on_pe[k]:
                     nc.tensor.matmul(
-                        mp[:], lhsT=rt[k, j // 4][:, j % 4, cols], rhs=vm[:, j // 4, j % 4:j % 4 + 1], start=(j == 0), stop=(j == 15)
+                        mbank[k][:],
+                        lhsT=vm[:, g, t:t + 1].to_broadcast([P, P]),
+                        rhs=rt[k, g][:, t, :],
+                        start=(g == 0 and t == on_pe[k][0]),
+                        stop=(g == GN - 1 and t == on_pe[k][-1]),
                     )
-                inv = work.tile([P, 1], F32, name="inv", tag="inv")
-                nc.vector.reciprocal(inv[:], mp[:])
-                for e in range(2):
-                    ecols = slice(KP * e, KP * (e + 1))
-                    ps = psum.tile([P, KP], F32, name="ps", tag="s")
-                    for g in range(GN):
-                        nc.tensor.matmul_mx(
-                            out=ps[:],
-                            lhsT=codes[g][:, cols].bitcast(FP8X4),
-                            lhsT_scale=planes[g][:, cols],
-                            rhs=zs[:, g, 2 * KP * e:2 * KP * (e + 1)].bitcast(FP4X4),
-                            rhs_scale=z_plane[:, g, ecols],
-                            start=(g == 0),
-                            stop=(g == GN - 1),
-                        )
-                    res = work.tile([P, KP], F32, name="res", tag="res", bufs=4)
-                    nc.vector.scalar_tensor_tensor(res[:], ps[:], inv[:], sq[i][:, ecols], MULT, ADD)
-                    nc.sync.dma_start(out=out_view[:, i, ecols], in_=res[:])
+
+        def mass_join(k):
+            nc.vector.scalar_tensor_tensor(mass_acc[k][:], mbank[k][:], 1.0 / P, mass_acc[k][:], MULT, ADD)
+
+        inv = {}
+        mcol = {}
+
+        def mass_col(k):
+            mcol[k] = psum.tile([P, 2], F32, name="mp", tag="t")
+            for s in range(2):
+                nc.tensor.matmul(mcol[k][:, s:s + 1], lhsT=mass_acc[k][:, P * s:P * (s + 1)], rhs=ones[:], start=True, stop=True)
+
+        def mass_inv(k):
+            inv[k] = work.tile([P, 2], F32, name="inv", tag="inv")
+            nc.vector.reciprocal(inv[k][:], mcol[k][:])
+
+        proj = {}
+
+        def stage2(i):
+            k, s = divmod(i, 2)
+            cols = slice(P * s, P * (s + 1))
+            for e in range(2):
+                ps = psum.tile([P, KP], F32, name="ps", tag="s")
+                for g in G_ORDER:
+                    nc.tensor.matmul_mx(
+                        out=ps[:],
+                        lhsT=codes[k, g][:, cols].bitcast(FP8X4),
+                        lhsT_scale=planes[k, g][:, cols],
+                        rhs=zs[:, g, 2 * KP * e:2 * KP * (e + 1)].bitcast(FP4X4),
+                        rhs_scale=z_plane[:, g, KP * e:KP * (e + 1)],
+                        start=(g == G_ORDER[0]),
+                        stop=(g == G_ORDER[-1]),
+                    )
+                proj[i, e] = ps
+
+        def finish(i, e):
+            ecols = slice(KP * e, KP * (e + 1))
+            res = work.tile([P, KP], F32, name="res", tag="res", bufs=4)
+            nc.vector.scalar_tensor_tensor(res[:], proj[i, e][:], inv[i // 2][:, i % 2:i % 2 + 1], sq[i][:, ecols], MULT, ADD)
+            nc.sync.dma_start(out=out_view[:, i, ecols], in_=res[:])
+
+        turn(3, 0, 0)
+        turn(3, 0, 1)
+        turn_outs(3, 0, "svsv")
+        turn(3, 1, 0)
+        turn(3, 1, 1)
+        turn_outs(3, 1, "svsv")
+        turn(3, 2, 0)
+        turn(3, 2, 1)
+        turn(3, 3, 0)
+        turn(3, 3, 1)
+        small = col_scale(0)
+        small[0]()
+        turn_out(3, 2, 0, "s")
+        turn_out(3, 2, 1, "v")
+        small[1]()
+        turn_out(3, 2, 2, "s")
+        turn_out(3, 2, 3, "v")
+        small[2]()
+        turn_out(3, 3, 0, "s")
+        turn_out(3, 3, 1, "v")
+        small[3]()
+        small[4]()
+        turn_out(3, 3, 2, "s")
+        turn_out(3, 3, 3, "v")
+        scale(0, 0)
+        scale(0, 1)
+        mass_t(0, (0, 1))
+        small = col_scale(1)
+        m0 = mass_v(0, 0) + mass_v(0, 1)
+        small[0]()
+        m0[0]()
+        small[1]()
+        m0[1]()
+        small[2]()
+        interleave(0, 0, "v")
+        small[3]()
+        small[4]()
+        scale(0, 2)
+        scale(0, 3)
+        mass_t(0, (2, 3))
+        m0 += mass_v(0, 2) + mass_v(0, 3)
+        quant(0, 0)
+        m0[2]()
+        interleave(0, 1, "v")
+        m0[3]()
+        quant(0, 1)
+        m0[4]()
+        interleave(0, 2, "v")
+        m0[5]()
+        quant(0, 2)
+        m0[6]()
+        interleave(0, 3, "v")
+        m0[7]()
+        quant(0, 3)
+        for op in m0[8:]:
+            op()
+        mass_join(0)
+        for k in range(NP):
+            more = k + 1 < NP
+            stage2(2 * k)
+            mass_col(k)
+            if more:
+                mass_t(k + 1, range(GN))
+            stage2(2 * k + 1)
+            if more:
+                n = k + 1
+                vi = 1
+                for g in range(GN):
+                    scale(n, g)
+                    if g >= vi + 1:
+                        interleave(n, g - 1, "s")
+                if vi < GN:
+                    interleave(n, GN - 1, "s")
+                ms = []
+                for g in range(GN):
+                    ms += mass_v(n, g)
+                others = [lambda g=g: interleave(n, g, "v") for g in range(vi)] + [
+                    lambda: quant(n, 0),
+                    lambda: quant(n, 1),
+                    lambda: mass_inv(k),
+                    lambda: finish(2 * k, 0),
+                    lambda: finish(2 * k, 1),
+                    lambda: quant(n, 2),
+                    lambda: finish(2 * k + 1, 0),
+                    lambda: quant(n, 3),
+                    lambda: finish(2 * k + 1, 1),
+                ]
+                order = []
+                for q in range(max(len(ms), len(others))):
+                    order += ms[q:q + 1] + others[q:q + 1]
+                for op in order:
+                    op()
+                mass_join(n)
+            else:
+                mass_inv(k)
+                for s in range(2):
+                    for e in range(2):
+                        finish(2 * k + s, e)

@@ -27,6 +27,9 @@ GN = N // KP
 NP = 4
 W = 256
 G_ORDER = (0, 1, 2, 3)
+SPLIT = (2, 3)
+TURN_FIRST = 4
+SUM_AT = 2
 
 
 def tile_sinkhorn_step_barycentre_f1_kernel(tc, x, y_words, y_scales, a, b, gain, z_words, z_scales, start, out):
@@ -40,11 +43,9 @@ def tile_sinkhorn_step_barycentre_f1_kernel(tc, x, y_words, y_scales, a, b, gain
         y_plane = keep.tile([P, GD, N], U8, name="y_plane", align_bytes=64)
         z_plane = keep.tile([P, GN, E], U8, name="z_plane", align_bytes=64)
         warm = keep.tile([P, 1], F32, name="warm")
-        ones = keep.tile([P, 1], F32, name="ones")
         ident = keep.tile([P, P], F32, name="ident")
         nc.vector.memset(y_plane[:].rearrange("p g n -> p (g n)").bitcast(I32), 0)
         nc.vector.memset(warm[:], 0.0)
-        nc.vector.memset(ones[:], 1.0)
         nc.vector.memset(z_plane[:].rearrange("p g n -> p (g n)").bitcast(I32), 0)
         make_identity(nc, ident[:])
         nc.scalar.activation(warm[:], warm[:], ACT.Exp)
@@ -88,12 +89,12 @@ def tile_sinkhorn_step_barycentre_f1_kernel(tc, x, y_words, y_scales, a, b, gain
         nc.sync.dma_start(out=a_sb[:], in_=a.rearrange("(p i) -> p i", i=MT))
         for i in range(3, MT):
             load_x(i)
+        for i in range(MT):
+            nc.sync.dma_start(out=st[i][:], in_=start_view[:, i, :])
         nc.sync.dma_start(out=b_sb[:], in_=b.rearrange("(g p t) -> p g t", p=P, t=4))
         nc.sync.dma_start(out=gain_sb[:], in_=gain.rearrange("(g p t) -> p g t", p=P, t=4))
         load_scales(z_plane, z_scales)
         nc.sync.dma_start(out=zs[:].bitcast(I32), in_=z_words.rearrange("g p n -> p g n").bitcast(I32))
-        for i in range(MT):
-            nc.sync.dma_start(out=st[i][:], in_=start_view[:, i, :])
 
         a_n = keep.tile([P, MT], F32, name="a_n")
         x_codes = {}
@@ -171,8 +172,7 @@ def tile_sinkhorn_step_barycentre_f1_kernel(tc, x, y_words, y_scales, a, b, gain
                 nc.gpsimd.tensor_scalar(kern[i][:], kern[i][:], rec[:], a_n[:, i:i + 1], MULT, MULT)
             else:
                 for g in range(GN):
-                    eng = nc.vector if g < 3 else nc.gpsimd
-                    eng.tensor_scalar(kern[i][:, g, :, :], kern[i][:, g, :, :], rec[:], a_n[:, i:i + 1], MULT, MULT)
+                    nc.vector.tensor_scalar(kern[i][:, g, :, :], kern[i][:, g, :, :], rec[:], a_n[:, i:i + 1], MULT, MULT)
 
         def turn_outs(k, g, engs):
             for j in range(4):
@@ -198,6 +198,12 @@ def tile_sinkhorn_step_barycentre_f1_kernel(tc, x, y_words, y_scales, a, b, gain
                 nc.vector.tensor_scalar(rt[k, g][:, j, :], src, 1.0, None, MULT, ADD, accum_out=acc)
             else:
                 nc.scalar.activation(rt[k, g][:, j, :], src, ACT.Copy, accum_out=acc)
+
+        def quarter(q):
+            if q < 4:
+                nc.gpsimd.tensor_scalar(sq[q][:], st[q][:], 0.25, 0.0, MULT, ADD)
+            else:
+                nc.vector.tensor_scalar(sq[q][:], st[q][:], 0.25, None, MULT)
 
         sq = [keep.tile([P, E], BF16, name="sq%d" % i) for i in range(MT)]
 
@@ -226,45 +232,38 @@ def tile_sinkhorn_step_barycentre_f1_kernel(tc, x, y_words, y_scales, a, b, gain
                 if i == 0 and c == 2:
                     x_quant(1)
             row_min(i)
+            if i + 2 < MT:
+                x_copy(i + 2)
+                x_quant(i + 2)
             if i == 0:
                 nc.vector.tensor_scalar(a_n[:], a_sb[:], float(N), None, MULT)
             if i >= 1:
                 row_scale(i - 1)
-            if i >= 4:
-                nc.gpsimd.tensor_scalar(sq[i - 4][:], st[i - 4][:], 0.25, 0.0, MULT, ADD)
-            if i + 2 < MT:
-                x_copy(i + 2)
+                if 3 <= i <= 6:
+                    quarter(i - 3)
             expo(i)
             for g in gs:
-                turn_outs(k, g, "vsvs" if i + 1 < MT else "vvvv")
-            if i + 2 < MT:
-                x_quant(i + 2)
+                turn_outs(k, g, ("vsvs" if g % 2 else "vsss") if i + 1 < MT else "vvvv")
         turn(2, 2, 0)
         turn(2, 2, 1)
         turn(2, 3, 0)
         turn(2, 3, 1)
-        turn_outs(2, 2, "vssv")
+        turn_outs(2, 2, "ssss")
+        turn_outs(2, 3, "ssss")
         row_scale(MT - 1)
-        turn_outs(2, 3, "ssvs")
 
         v = keep.tile([P, GN, 4], F32, name="v")
         vg = keep.tile([P, GN, 4], F32, name="vg")
-        vm = keep.tile([P, GN, 4], F32, name="vm")
         tot = keep.tile([P, GN, 4], F32, name="tot")
         rtot = keep.tile([P, GN, 4], F32, name="rtot")
 
-        def col_scale(h):
-            gs = slice(2 * h, 2 * h + 2)
+        def col_scale():
             return [
-                lambda: nc.vector.tensor_reduce(tot[:, gs, :], csum[:, gs, :, :], AX, ADD),
-                lambda: nc.vector.reciprocal(rtot[:, gs, :], tot[:, gs, :]),
-                lambda: nc.vector.scalar_tensor_tensor(v[:, gs, :], rtot[:, gs, :], float(M), b_sb[:, gs, :], MULT, MULT),
-                lambda: nc.vector.tensor_tensor(vg[:, gs, :], v[:, gs, :], gain_sb[:, gs, :], MULT),
-                lambda: nc.vector.tensor_scalar(vm[:, gs, :], v[:, gs, :], 1.0 / (0.75 * N), None, MULT),
+                lambda: nc.vector.tensor_reduce(tot[:], csum[:], AX, ADD),
+                lambda: nc.vector.reciprocal(rtot[:], tot[:]),
+                lambda: nc.vector.scalar_tensor_tensor(v[:], rtot[:], float(M), b_sb[:], MULT, MULT),
+                lambda: nc.vector.tensor_tensor(vg[:], v[:], gain_sb[:], MULT),
             ]
-
-        for q in range(4, MT):
-            nc.gpsimd.tensor_scalar(sq[q][:], st[q][:], 0.25, 0.0, MULT, ADD)
 
         gb = {}
         gi = {}
@@ -275,6 +274,12 @@ def tile_sinkhorn_step_barycentre_f1_kernel(tc, x, y_words, y_scales, a, b, gain
             gb[k, g] = work.tile([P, 4, W], BF16, name="gb", tag="gb", bufs=5)
             for t in range(4):
                 nc.scalar.activation(gb[k, g][:, t, :], rt[k, g][:, t, :], ACT.Copy, scale=vg[:, g, t:t + 1])
+
+        def direct(k, g):
+            gi[k, g] = work.tile([P, W, 4], BF16, name="gi", tag="gi", bufs=5, align_bytes=64)
+            nc.vector.tensor_tensor(
+                gi[k, g][:], rt[k, g][:].rearrange("p t m -> p m t"), vg[:, g, :].unsqueeze(1).to_broadcast([P, W, 4]), MULT
+            )
 
         def interleave(k, g, eng):
             gi[k, g] = work.tile([P, W, 4], BF16, name="gi", tag="gi", bufs=5, align_bytes=64)
@@ -292,50 +297,42 @@ def tile_sinkhorn_step_barycentre_f1_kernel(tc, x, y_words, y_scales, a, b, gain
                 out=codes[k, g][:].bitcast(FP8X4), scales=planes[k, g][:], in_=gi[k, g][:].rearrange("p m t -> p (m t)")
             )
 
-        mass_acc = {}
-        mbank = {}
-        on_pe = {0: (3,), 1: (3,), 2: (3,), 3: (3,)}
+        pt = {}
 
-        def mass_v(k, g):
-            ops = []
+        def weigh(k, g):
+            if g % 2 == 0:
+                pt[k, g // 2] = work.tile([P, 2, 4, W], F32, name="pt", tag="kern", bufs=5)
             for t in range(4):
-                if t in on_pe[k]:
-                    continue
-                src, scl = rt[k, g][:, t, :], vm[:, g, t:t + 1]
-                if k not in mass_acc:
-                    mass_acc[k] = work.tile([P, W], F32, name="macc", tag="macc", bufs=2)
-                    ops.append(lambda src=src, scl=scl: nc.vector.tensor_scalar(mass_acc[k][:], src, scl, None, MULT))
-                else:
-                    ops.append(lambda src=src, scl=scl: nc.vector.scalar_tensor_tensor(mass_acc[k][:], src, scl, mass_acc[k][:], MULT, ADD))
-            return ops
+                nc.scalar.activation(pt[k, g // 2][:, g % 2, t, :], rt[k, g][:, t, :], ACT.Copy, scale=v[:, g, t:t + 1])
 
-        def mass_t(k, gs):
-            if k not in mbank:
-                mbank[k] = psum.tile([P, W], F32, name="mb", tag="t")
-            for g in gs:
-                for t in on_pe[k]:
+        mbank = {}
+
+        def mass_turn(k):
+            mbank[k] = psum.tile([P, 2, P], F32, name="mb", tag="t")
+            for s in range(2):
+                for j in range(16):
+                    g, t = divmod(j, 4)
                     nc.tensor.matmul(
-                        mbank[k][:],
-                        lhsT=vm[:, g, t:t + 1].to_broadcast([P, P]),
-                        rhs=rt[k, g][:, t, :],
-                        start=(g == 0 and t == on_pe[k][0]),
-                        stop=(g == GN - 1 and t == on_pe[k][-1]),
+                        mbank[k][:, s, :],
+                        lhsT=pt[k, g // 2][:, g % 2, t, P * s:P * (s + 1)],
+                        rhs=ident[:],
+                        is_transpose=True,
+                        start=(j == 0),
+                        stop=(j == 15),
                     )
 
-        def mass_join(k):
-            nc.vector.scalar_tensor_tensor(mass_acc[k][:], mbank[k][:], 1.0 / P, mass_acc[k][:], MULT, ADD)
-
         inv = {}
-        mcol = {}
+        mrow = {}
 
-        def mass_col(k):
-            mcol[k] = psum.tile([P, 2], F32, name="mp", tag="t")
+        def mass_sum(k):
+            mrow[k] = work.tile([P, 2], F32, name="mrow", tag="mrow")
             for s in range(2):
-                nc.tensor.matmul(mcol[k][:, s:s + 1], lhsT=mass_acc[k][:, P * s:P * (s + 1)], rhs=ones[:], start=True, stop=True)
+                junk = work.tile([P, P], BF16, name="junk", tag="junk")
+                nc.scalar.activation(junk[:], mbank[k][:, s, :], ACT.Copy, scale=1.0 / (0.75 * N), accum_out=mrow[k][:, s:s + 1])
 
         def mass_inv(k):
             inv[k] = work.tile([P, 2], F32, name="inv", tag="inv")
-            nc.vector.reciprocal(inv[k][:], mcol[k][:])
+            nc.vector.reciprocal(inv[k][:], mrow[k][:])
 
         proj = {}
 
@@ -372,91 +369,55 @@ def tile_sinkhorn_step_barycentre_f1_kernel(tc, x, y_words, y_scales, a, b, gain
         turn(3, 2, 1)
         turn(3, 3, 0)
         turn(3, 3, 1)
-        small = col_scale(0)
-        small[0]()
-        turn_out(3, 2, 0, "s")
-        turn_out(3, 2, 1, "v")
-        small[1]()
-        turn_out(3, 2, 2, "s")
-        turn_out(3, 2, 3, "v")
-        small[2]()
-        turn_out(3, 3, 0, "s")
-        turn_out(3, 3, 1, "v")
-        small[3]()
-        small[4]()
-        turn_out(3, 3, 2, "s")
-        turn_out(3, 3, 3, "v")
-        scale(0, 0)
-        scale(0, 1)
-        mass_t(0, (0, 1))
-        small = col_scale(1)
-        m0 = mass_v(0, 0) + mass_v(0, 1)
-        small[0]()
-        m0[0]()
-        small[1]()
-        m0[1]()
-        small[2]()
-        interleave(0, 0, "v")
-        small[3]()
-        small[4]()
-        scale(0, 2)
-        scale(0, 3)
-        mass_t(0, (2, 3))
-        m0 += mass_v(0, 2) + mass_v(0, 3)
+        turn_outs(3, 2, "svsv")
+        turn_outs(3, 3, "svsv")
+        small = col_scale()
+        for q in range(4):
+            small[q]()
+            quarter(4 + q)
+        for g in range(GN):
+            weigh(0, g)
+        direct(0, 0)
+        direct(0, 1)
         quant(0, 0)
-        m0[2]()
-        interleave(0, 1, "v")
-        m0[3]()
+        direct(0, 2)
         quant(0, 1)
-        m0[4]()
-        interleave(0, 2, "v")
-        m0[5]()
+        direct(0, 3)
         quant(0, 2)
-        m0[6]()
-        interleave(0, 3, "v")
-        m0[7]()
         quant(0, 3)
-        for op in m0[8:]:
-            op()
-        mass_join(0)
-        for k in range(NP):
-            more = k + 1 < NP
+        for n in range(1, NP + 1):
+            k = n - 1
+            if k < TURN_FIRST:
+                mass_turn(k)
             stage2(2 * k)
-            mass_col(k)
-            if more:
-                mass_t(k + 1, range(GN))
+            if k >= TURN_FIRST:
+                mass_turn(k)
             stage2(2 * k + 1)
-            if more:
-                n = k + 1
-                vi = 1
+            if n in SPLIT:
+                scale(n, 3)
+                interleave(n, 3, "s")
+            if n == NP:
+                mass_sum(k)
+            if n < NP:
                 for g in range(GN):
-                    scale(n, g)
-                    if g >= vi + 1:
-                        interleave(n, g - 1, "s")
-                if vi < GN:
-                    interleave(n, GN - 1, "s")
-                ms = []
-                for g in range(GN):
-                    ms += mass_v(n, g)
-                others = [lambda g=g: interleave(n, g, "v") for g in range(vi)] + [
-                    lambda: quant(n, 0),
-                    lambda: quant(n, 1),
-                    lambda: mass_inv(k),
-                    lambda: finish(2 * k, 0),
-                    lambda: finish(2 * k, 1),
-                    lambda: quant(n, 2),
-                    lambda: finish(2 * k + 1, 0),
-                    lambda: quant(n, 3),
-                    lambda: finish(2 * k + 1, 1),
-                ]
-                order = []
-                for q in range(max(len(ms), len(others))):
-                    order += ms[q:q + 1] + others[q:q + 1]
-                for op in order:
-                    op()
-                mass_join(n)
+                    if g == SUM_AT:
+                        mass_sum(k)
+                    weigh(n, g)
+                direct(n, 0)
+                direct(n, 1)
+                quant(n, 0)
+                mass_inv(k)
+                finish(2 * k, 0)
+                direct(n, 2)
+                quant(n, 1)
+                finish(2 * k, 1)
+                if n not in SPLIT:
+                    direct(n, 3)
+                quant(n, 2)
+                finish(2 * k + 1, 0)
+                quant(n, 3)
+                finish(2 * k + 1, 1)
             else:
                 mass_inv(k)
-                for s in range(2):
-                    for e in range(2):
-                        finish(2 * k + s, e)
+                for q in range(4):
+                    finish(2 * k + q // 2, q % 2)

@@ -4,6 +4,8 @@ import concourse.mybir as mybir
 from concourse.masks import make_identity
 
 M, D, N, E = 1024, 1024, 2048, 1024
+EPS = 0.8
+TAU = 0.75
 FLOPS = 2 * M * D * N + 2 * M * N * E
 
 F32 = mybir.dt.float32
@@ -16,20 +18,22 @@ FP4X4 = mybir.dt.float4_e2m1fn_x4
 ADD = mybir.AluOpType.add
 MULT = mybir.AluOpType.mult
 MIN = mybir.AluOpType.min
-AX = mybir.AxisListType.X
-ACT = mybir.ActivationFunctionType
+X = mybir.AxisListType.X
+EXP = mybir.ActivationFunctionType.Exp
+COPY = mybir.ActivationFunctionType.Copy
 
 P = 128
-KP = 512
-MT = M // P
-GD = D // KP
+T = 4
+KP = P * T
+TILES = M // P
+XG = D // KP
 GN = N // KP
-NP = 4
-W = 256
-G_ORDER = (0, 1, 2, 3)
-SPLIT = (2, 3)
-TURN_FIRST = 4
-SUM_AT = 2
+PAIRS = TILES // 2
+W = 2 * P
+HALVES = E // KP
+
+OUT_EVEN, OUT_ODD = "vsss", "vsvs"
+SCALAR_GROUP = (2, 3)
 
 
 def tile_sinkhorn_step_barycentre_f1_kernel(tc, x, y_words, y_scales, a, b, gain, z_words, z_scales, start, out):
@@ -40,7 +44,13 @@ def tile_sinkhorn_step_barycentre_f1_kernel(tc, x, y_words, y_scales, a, b, gain
         psum = ctx.enter_context(tc.psum_pool(name="psum", bufs=4))
         ctx.enter_context(tc.manual_schedule())
 
-        y_plane = keep.tile([P, GD, N], U8, name="y_plane", align_bytes=64)
+        def mx_bank(name):
+            return psum.tile([P, KP], F32, name=name, tag="mx", bufs=3)
+
+        def turn_bank(shape, name):
+            return psum.tile(shape, F32, name=name, tag="turn", bufs=5)
+
+        y_plane = keep.tile([P, XG, N], U8, name="y_plane", align_bytes=64)
         z_plane = keep.tile([P, GN, E], U8, name="z_plane", align_bytes=64)
         warm = keep.tile([P, 1], F32, name="warm")
         ident = keep.tile([P, P], F32, name="ident")
@@ -48,35 +58,32 @@ def tile_sinkhorn_step_barycentre_f1_kernel(tc, x, y_words, y_scales, a, b, gain
         nc.vector.memset(warm[:], 0.0)
         nc.vector.memset(z_plane[:].rearrange("p g n -> p (g n)").bitcast(I32), 0)
         make_identity(nc, ident[:])
-        nc.scalar.activation(warm[:], warm[:], ACT.Exp)
+        nc.scalar.activation(warm[:], warm[:], EXP)
 
-        x_view = x.rearrange("(p i) d -> p i d", i=MT)
-        start_view = start.rearrange("(p i) e -> p i e", i=MT)
-        out_view = out.rearrange("(p i) e -> p i e", i=MT)
+        x_view = x.rearrange("(p i) d -> p i d", i=TILES)
+        start_view = start.rearrange("(p i) e -> p i e", i=TILES)
+        out_view = out.rearrange("(p i) e -> p i e", i=TILES)
 
-        xs = [keep.tile([P, D], BF16, name="x%d" % i, align_bytes=64) for i in range(MT)]
-        ys = [keep.tile([P, GD, 2 * KP], U8, name="y%d" % c, align_bytes=64) for c in range(GN)]
-        zs = keep.tile([P, GN, 2 * E], U8, name="zs", align_bytes=64)
-        st = [keep.tile([P, E], BF16, name="st%d" % i) for i in range(MT)]
-        a_sb = keep.tile([P, MT], BF16, name="a_sb")
-        b_sb = keep.tile([P, GN, 4], BF16, name="b_sb")
-        gain_sb = keep.tile([P, GN, 4], BF16, name="gain_sb")
+        x_rows = [keep.tile([P, D], BF16, name="x_rows%d" % i, align_bytes=64) for i in range(TILES)]
+        y_codes = [keep.tile([P, XG, 2 * KP], U8, name="y_codes%d" % g, align_bytes=64) for g in range(GN)]
+        z_codes = keep.tile([P, GN, 2 * E], U8, name="z_codes", align_bytes=64)
+        starts = [keep.tile([P, E], BF16, name="starts%d" % i) for i in range(TILES)]
+        quarters = [keep.tile([P, E], BF16, name="quarters%d" % i) for i in range(TILES)]
+        a_sb = keep.tile([P, TILES], BF16, name="a_sb")
+        b_sb = keep.tile([P, GN, T], BF16, name="b_sb")
+        gain_sb = keep.tile([P, GN, T], BF16, name="gain_sb")
 
         def load_x(i):
-            nc.sync.dma_start(out=xs[i][:], in_=x_view[:, i, :])
+            nc.sync.dma_start(out=x_rows[i][:], in_=x_view[:, i, :])
 
-        def load_y(c):
-            nc.sync.dma_start(
-                out=ys[c][:].bitcast(I32),
-                in_=y_words[:, :, 2 * KP * c:2 * KP * (c + 1)].rearrange("g p n -> p g n").bitcast(I32),
-            )
+        def load_y(g):
+            cols = slice(2 * KP * g, 2 * KP * (g + 1))
+            nc.sync.dma_start(out=y_codes[g][:].bitcast(I32), in_=y_words[:, :, cols].rearrange("g p n -> p g n").bitcast(I32))
 
         def load_scales(plane, scales):
             for q in range(4):
-                nc.sync.dma_start(
-                    out=plane[32 * q:32 * q + 4, :, :].bitcast(I32),
-                    in_=scales[:, 4 * q:4 * q + 4, :].rearrange("g r n -> r g n").bitcast(I32),
-                )
+                rows = scales[:, 4 * q:4 * q + 4, :].rearrange("g r n -> r g n")
+                nc.sync.dma_start(out=plane[32 * q:32 * q + 4, :, :].bitcast(I32), in_=rows.bitcast(I32))
 
         load_x(0)
         load_scales(y_plane, y_scales)
@@ -86,153 +93,132 @@ def tile_sinkhorn_step_barycentre_f1_kernel(tc, x, y_words, y_scales, a, b, gain
         load_y(2)
         load_y(3)
         load_x(2)
-        nc.sync.dma_start(out=a_sb[:], in_=a.rearrange("(p i) -> p i", i=MT))
-        for i in range(3, MT):
+        nc.sync.dma_start(out=a_sb[:], in_=a.rearrange("(p i) -> p i", i=TILES))
+        for i in range(3, TILES):
             load_x(i)
-        for i in range(MT):
-            nc.sync.dma_start(out=st[i][:], in_=start_view[:, i, :])
-        nc.sync.dma_start(out=b_sb[:], in_=b.rearrange("(g p t) -> p g t", p=P, t=4))
-        nc.sync.dma_start(out=gain_sb[:], in_=gain.rearrange("(g p t) -> p g t", p=P, t=4))
+        for i in range(TILES):
+            nc.sync.dma_start(out=starts[i][:], in_=start_view[:, i, :])
+        nc.sync.dma_start(out=b_sb[:], in_=b.rearrange("(g p t) -> p g t", p=P, t=T))
+        nc.sync.dma_start(out=gain_sb[:], in_=gain.rearrange("(g p t) -> p g t", p=P, t=T))
         load_scales(z_plane, z_scales)
-        nc.sync.dma_start(out=zs[:].bitcast(I32), in_=z_words.rearrange("g p n -> p g n").bitcast(I32))
+        nc.sync.dma_start(out=z_codes[:].bitcast(I32), in_=z_words.rearrange("g p n -> p g n").bitcast(I32))
 
-        a_n = keep.tile([P, MT], F32, name="a_n")
+        x_turned = {}
+        x_grouped = {}
         x_codes = {}
         x_planes = {}
-        x_words = {}
 
         def x_turn(i):
-            words = xs[i][:].bitcast(F32)
-            xt = psum.tile([P, GD, 2, P], F32, name="xt", tag="t")
-            for g in range(GD):
+            words = x_rows[i][:].bitcast(F32)
+            x_turned[i] = turn_bank([P, XG, 2, P], "x_turned")
+            for g in range(XG):
                 for u in range(2):
-                    nc.tensor.transpose(xt[:, g, u, :], words[:, 256 * g + u:256 * (g + 1):2], ident[:])
-            x_words[i] = xt
+                    nc.tensor.transpose(x_turned[i][:, g, u, :], words[:, 2 * P * g + u:2 * P * (g + 1):2], ident[:])
 
         def x_copy(i):
-            xg = work.tile([P, GD, P, 4], BF16, name="xg", align_bytes=64)
-            dst = xg[:].rearrange("p g r t -> p g (r t)").bitcast(F32).rearrange("p g (r u) -> p g r u", u=2)
-            nc.scalar.copy(dst, x_words[i][:].rearrange("p g u r -> p g r u"))
-            x_words[i] = xg
+            x_grouped[i] = work.tile([P, XG, P, T], BF16, name="x_grouped", align_bytes=64)
+            dst = x_grouped[i][:].rearrange("p g r t -> p g (r t)").bitcast(F32).rearrange("p g (r u) -> p g r u", u=2)
+            nc.scalar.copy(dst, x_turned[i][:].rearrange("p g u r -> p g r u"))
 
         def x_quant(i):
-            codes = keep.tile([P, GD, P], U32, name="x_codes%d" % i, align_bytes=64)
-            plane = keep.tile([P, GD, P], U8, name="x_plane%d" % i, align_bytes=64)
+            x_codes[i] = keep.tile([P, XG, P], U32, name="x_codes%d" % i, align_bytes=64)
+            x_planes[i] = keep.tile([P, XG, P], U8, name="x_planes%d" % i, align_bytes=64)
             nc.vector.quantize_mx(
-                out=codes[:].rearrange("p g r -> p (g r)").bitcast(FP8X4),
-                scales=plane[:].rearrange("p g r -> p (g r)"),
-                in_=x_words[i][:].rearrange("p g r t -> p (g r t)"),
+                out=x_codes[i][:].rearrange("p g r -> p (g r)").bitcast(FP8X4),
+                scales=x_planes[i][:].rearrange("p g r -> p (g r)"),
+                in_=x_grouped[i][:].rearrange("p g r t -> p (g r t)"),
             )
-            x_codes[i] = codes
-            x_planes[i] = plane
 
+        sums = {}
         kern = {}
         mins = {}
         shift = {}
-        banks = {}
+        row_sum = {}
 
-        def sim_mm(i, c):
-            ps = psum.tile([P, KP], F32, name="ps", tag="s")
-            for g in range(GD):
+        def similarity(i, g):
+            sums[i, g] = mx_bank("sums")
+            for d in range(XG):
                 nc.tensor.matmul_mx(
-                    out=ps[:],
-                    lhsT=x_codes[i][:, g, :].bitcast(FP8X4),
-                    lhsT_scale=x_planes[i][:, g, :],
-                    rhs=ys[c][:, g, :].bitcast(FP4X4),
-                    rhs_scale=y_plane[:, g, KP * c:KP * (c + 1)],
-                    start=(g == 0),
-                    stop=(g == GD - 1),
+                    out=sums[i, g][:],
+                    lhsT=x_codes[i][:, d, :].bitcast(FP8X4),
+                    lhsT_scale=x_planes[i][:, d, :],
+                    rhs=y_codes[g][:, d, :].bitcast(FP4X4),
+                    rhs_scale=y_plane[:, d, KP * g:KP * (g + 1)],
+                    start=(d == 0),
+                    stop=(d == XG - 1),
                 )
-            banks[i, c] = ps
 
-        def sim_out(i, c):
-            if c == 0:
-                kern[i] = work.tile([P, GN, 4, P], F32, name="kern", tag="kern", bufs=5)
-                mins[i] = work.tile([P, GN], F32, name="mins", tag="mins")
-            nc.vector.tensor_scalar(
-                kern[i][:, c, :, :], banks[i, c][:].rearrange("m (p t) -> m t p", t=4), -1.25, None, MULT, MIN, accum_out=mins[i][:, c:c + 1]
-            )
+        def take_out(i, g):
+            if g == 0:
+                kern[i] = work.tile([P, GN, T, P], F32, name="kern", tag="kern", bufs=5)
+                mins[i] = work.tile([P, GN], F32, name="mins")
+            by_slot = sums[i, g][:].rearrange("r (p t) -> r t p", t=T)
+            nc.vector.tensor_scalar(kern[i][:, g, :, :], by_slot, -1.0 / EPS, None, MULT, MIN, accum_out=mins[i][:, g:g + 1])
 
         def row_min(i):
-            sh = work.tile([P, 1], F32, name="sh", tag="sh")
-            nc.vector.tensor_reduce(sh[:], mins[i][:], AX, MIN)
-            shift[i] = sh
+            shift[i] = work.tile([P, 1], F32, name="shift")
+            nc.vector.tensor_reduce(shift[i][:], mins[i][:], X, MIN)
 
-        rsum = {}
+        def exponential(i):
+            row_sum[i] = work.tile([P, 1], F32, name="row_sum")
+            nc.scalar.activation(kern[i][:], kern[i][:], EXP, bias=shift[i][:], scale=-1.0, accum_out=row_sum[i][:])
 
-        def expo(i):
-            rs = work.tile([P, 1], F32, name="rs", tag="rs")
-            nc.scalar.activation(kern[i][:], kern[i][:], ACT.Exp, bias=shift[i][:], scale=-1.0, accum_out=rs[:])
-            rsum[i] = rs
+        a_n = keep.tile([P, TILES], F32, name="a_n")
 
         def row_scale(i):
-            rec = work.tile([P, 1], F32, name="rec", tag="rec")
-            nc.vector.reciprocal(rec[:], rsum[i][:])
-            if i < MT - 1:
-                nc.gpsimd.tensor_scalar(kern[i][:], kern[i][:], rec[:], a_n[:, i:i + 1], MULT, MULT)
+            recip = work.tile([P, 1], F32, name="recip")
+            nc.vector.reciprocal(recip[:], row_sum[i][:])
+            if i + 1 < TILES:
+                nc.gpsimd.tensor_scalar(kern[i][:], kern[i][:], recip[:], a_n[:, i:i + 1], MULT, MULT)
             else:
                 for g in range(GN):
-                    nc.vector.tensor_scalar(kern[i][:, g, :, :], kern[i][:, g, :, :], rec[:], a_n[:, i:i + 1], MULT, MULT)
+                    nc.vector.tensor_scalar(kern[i][:, g, :, :], kern[i][:, g, :, :], recip[:], a_n[:, i:i + 1], MULT, MULT)
 
-        def turn_outs(k, g, engs):
-            for j in range(4):
-                turn_out(k, g, j, engs[j])
+        def quarter(i, engine):
+            engine.tensor_scalar(quarters[i][:], starts[i][:], 1.0 - TAU, 0.0, MULT, ADD)
 
-        rt = {}
-        tb = {}
-        csum = keep.tile([P, GN, 4, NP], F32, name="csum")
+        turned = {}
+        banks = {}
+        col_parts = keep.tile([P, GN, T, PAIRS], F32, name="col_parts")
 
-        def turn(k, g, tt):
-            bank = psum.tile([P, 2, 2, P], F32, name="bank", tag="t")
-            for t in range(2):
-                for s in range(2):
-                    nc.tensor.transpose(bank[:, t, s, :], kern[2 * k + s][:, g, 2 * tt + t, :], ident[:])
-            tb[k, g, tt] = bank
+        def turn(k, g):
+            for h in range(2):
+                banks[k, g, h] = turn_bank([P, 2, 2, P], "banks")
+                for t in range(2):
+                    for s in range(2):
+                        nc.tensor.transpose(banks[k, g, h][:, t, s, :], kern[2 * k + s][:, g, 2 * h + t, :], ident[:])
 
-        def turn_out(k, g, j, eng):
-            if (k, g) not in rt:
-                rt[k, g] = keep.tile([P, 4, W], F32, name="rt%d_%d" % (k, g))
-            acc = csum[:, g, j, k:k + 1]
-            src = tb[k, g, j // 2][:, j % 2, :, :].rearrange("p s m -> p (s m)")
-            if eng == "v":
-                nc.vector.tensor_scalar(rt[k, g][:, j, :], src, 1.0, None, MULT, ADD, accum_out=acc)
-            else:
-                nc.scalar.activation(rt[k, g][:, j, :], src, ACT.Copy, accum_out=acc)
-
-        def quarter(q):
-            if q < 4:
-                nc.gpsimd.tensor_scalar(sq[q][:], st[q][:], 0.25, 0.0, MULT, ADD)
-            else:
-                nc.vector.tensor_scalar(sq[q][:], st[q][:], 0.25, None, MULT)
-
-        sq = [keep.tile([P, E], BF16, name="sq%d" % i) for i in range(MT)]
-
-        def turn_outs(k, g, engs):
-            for j in range(4):
-                turn_out(k, g, j, engs[j])
+        def turn_out(k, g, engines):
+            turned[k, g] = keep.tile([P, T, W], F32, name="turned%d_%d" % (k, g))
+            for t in range(T):
+                src = banks[k, g, t // 2][:, t % 2, :, :].rearrange("p s r -> p (s r)")
+                part = col_parts[:, g, t, k:k + 1]
+                if engines[t] == "v":
+                    nc.vector.tensor_scalar(turned[k, g][:, t, :], src, 1.0, None, MULT, ADD, accum_out=part)
+                else:
+                    nc.scalar.activation(turned[k, g][:, t, :], src, COPY, accum_out=part)
 
         x_turn(0)
         x_copy(0)
         x_quant(0)
-        for i in range(MT):
+        for i in range(TILES):
             k, half = divmod(i - 3, 2)
-            gs = (2 * half, 2 * half + 1) if i >= 3 else ()
-            for c in range(GN):
-                sim_mm(i, c)
-                if i == 0 and c == 1:
+            groups = (2 * half, 2 * half + 1) if i >= 3 else ()
+            for g in range(GN):
+                similarity(i, g)
+                if i == 0 and g == 1:
                     x_turn(1)
                     x_copy(1)
-            if i + 2 < MT:
+            if i + 2 < TILES:
                 x_turn(i + 2)
-            for g in gs:
-                turn(k, g, 0)
-                turn(k, g, 1)
-            for c in range(GN):
-                sim_out(i, c)
-                if i == 0 and c == 2:
+            for g in groups:
+                turn(k, g)
+            for g in range(GN):
+                take_out(i, g)
+                if i == 0 and g == 2:
                     x_quant(1)
             row_min(i)
-            if i + 2 < MT:
+            if i + 2 < TILES:
                 x_copy(i + 2)
                 x_quant(i + 2)
             if i == 0:
@@ -240,184 +226,169 @@ def tile_sinkhorn_step_barycentre_f1_kernel(tc, x, y_words, y_scales, a, b, gain
             if i >= 1:
                 row_scale(i - 1)
                 if 3 <= i <= 6:
-                    quarter(i - 3)
-            expo(i)
-            for g in gs:
-                turn_outs(k, g, ("vsvs" if g % 2 else "vsss") if i + 1 < MT else "vvvv")
-        turn(2, 2, 0)
-        turn(2, 2, 1)
-        turn(2, 3, 0)
-        turn(2, 3, 1)
-        turn_outs(2, 2, "ssss")
-        turn_outs(2, 3, "ssss")
-        row_scale(MT - 1)
+                    quarter(i - 3, nc.gpsimd)
+            exponential(i)
+            for g in groups:
+                turn_out(k, g, "vvvv" if i + 1 == TILES else OUT_ODD if g % 2 else OUT_EVEN)
 
-        v = keep.tile([P, GN, 4], F32, name="v")
-        vg = keep.tile([P, GN, 4], F32, name="vg")
-        tot = keep.tile([P, GN, 4], F32, name="tot")
-        rtot = keep.tile([P, GN, 4], F32, name="rtot")
+        turn(2, 2)
+        turn(2, 3)
+        turn_out(2, 2, "ssss")
+        turn_out(2, 3, "ssss")
+        row_scale(TILES - 1)
+        turn(3, 0)
+        turn_out(3, 0, "svsv")
+        turn(3, 1)
+        turn_out(3, 1, "svsv")
+        turn(3, 2)
+        turn(3, 3)
+        turn_out(3, 2, "svsv")
+        turn_out(3, 3, "svsv")
 
-        def col_scale():
-            return [
-                lambda: nc.vector.tensor_reduce(tot[:], csum[:], AX, ADD),
-                lambda: nc.vector.reciprocal(rtot[:], tot[:]),
-                lambda: nc.vector.scalar_tensor_tensor(v[:], rtot[:], float(M), b_sb[:], MULT, MULT),
-                lambda: nc.vector.tensor_tensor(vg[:], v[:], gain_sb[:], MULT),
-            ]
+        col_sum = keep.tile([P, GN, T], F32, name="col_sum")
+        col_recip = keep.tile([P, GN, T], F32, name="col_recip")
+        v = keep.tile([P, GN, T], F32, name="v")
+        v_gain = keep.tile([P, GN, T], F32, name="v_gain")
+        nc.vector.tensor_reduce(col_sum[:], col_parts[:], X, ADD)
+        quarter(4, nc.vector)
+        nc.vector.reciprocal(col_recip[:], col_sum[:])
+        quarter(5, nc.vector)
+        nc.vector.scalar_tensor_tensor(v[:], col_recip[:], float(M), b_sb[:], MULT, MULT)
+        quarter(6, nc.vector)
+        nc.vector.tensor_tensor(v_gain[:], v[:], gain_sb[:], MULT)
+        quarter(7, nc.vector)
 
-        gb = {}
-        gi = {}
-        codes = {}
-        planes = {}
-
-        def scale(k, g):
-            gb[k, g] = work.tile([P, 4, W], BF16, name="gb", tag="gb", bufs=5)
-            for t in range(4):
-                nc.scalar.activation(gb[k, g][:, t, :], rt[k, g][:, t, :], ACT.Copy, scale=vg[:, g, t:t + 1])
-
-        def direct(k, g):
-            gi[k, g] = work.tile([P, W, 4], BF16, name="gi", tag="gi", bufs=5, align_bytes=64)
-            nc.vector.tensor_tensor(
-                gi[k, g][:], rt[k, g][:].rearrange("p t m -> p m t"), vg[:, g, :].unsqueeze(1).to_broadcast([P, W, 4]), MULT
-            )
-
-        def interleave(k, g, eng):
-            gi[k, g] = work.tile([P, W, 4], BF16, name="gi", tag="gi", bufs=5, align_bytes=64)
-            dst = gi[k, g][:].rearrange("p (c i) t -> p c t i", i=4)
-            src = gb[k, g][:].rearrange("p t (c i) -> p c t i", i=4)
-            if eng == "s":
-                nc.scalar.copy(dst, src)
-            else:
-                nc.vector.tensor_copy(dst, src)
-
-        def quant(k, g):
-            codes[k, g] = work.tile([P, W], U32, name="cd", tag="cd", bufs=8, align_bytes=64)
-            planes[k, g] = work.tile([P, W], U8, name="pl", tag="pl", bufs=8, align_bytes=64)
-            nc.vector.quantize_mx(
-                out=codes[k, g][:].bitcast(FP8X4), scales=planes[k, g][:], in_=gi[k, g][:].rearrange("p m t -> p (m t)")
-            )
-
-        pt = {}
+        plan = {}
+        mass_parts = {}
+        mass = {}
+        inv = {}
 
         def weigh(k, g):
             if g % 2 == 0:
-                pt[k, g // 2] = work.tile([P, 2, 4, W], F32, name="pt", tag="kern", bufs=5)
-            for t in range(4):
-                nc.scalar.activation(pt[k, g // 2][:, g % 2, t, :], rt[k, g][:, t, :], ACT.Copy, scale=v[:, g, t:t + 1])
+                plan[k, g // 2] = work.tile([P, 2, T, W], F32, name="plan", tag="kern", bufs=5)
+            for t in range(T):
+                nc.scalar.activation(plan[k, g // 2][:, g % 2, t, :], turned[k, g][:, t, :], COPY, scale=v[:, g, t:t + 1])
 
-        mbank = {}
-
-        def mass_turn(k):
-            mbank[k] = psum.tile([P, 2, P], F32, name="mb", tag="t")
-            for s in range(2):
-                for j in range(16):
-                    g, t = divmod(j, 4)
-                    nc.tensor.matmul(
-                        mbank[k][:, s, :],
-                        lhsT=pt[k, g // 2][:, g % 2, t, P * s:P * (s + 1)],
-                        rhs=ident[:],
-                        is_transpose=True,
-                        start=(j == 0),
-                        stop=(j == 15),
-                    )
-
-        inv = {}
-        mrow = {}
+        def mass_turn(k, s):
+            mass_parts[k, s] = turn_bank([P, P], "mass_parts")
+            for q in range(GN * T):
+                g, t = divmod(q, T)
+                nc.tensor.matmul(
+                    mass_parts[k, s][:],
+                    lhsT=plan[k, g // 2][:, g % 2, t, P * s:P * (s + 1)],
+                    rhs=ident[:],
+                    is_transpose=True,
+                    start=(q == 0),
+                    stop=(q == GN * T - 1),
+                )
 
         def mass_sum(k):
-            mrow[k] = work.tile([P, 2], F32, name="mrow", tag="mrow")
             for s in range(2):
-                junk = work.tile([P, P], BF16, name="junk", tag="junk")
-                nc.scalar.activation(junk[:], mbank[k][:, s, :], ACT.Copy, scale=1.0 / (0.75 * N), accum_out=mrow[k][:, s:s + 1])
+                mass[k, s] = work.tile([P, 1], F32, name="mass")
+                unused = work.tile([P, P], BF16, name="unused")
+                nc.scalar.activation(unused[:], mass_parts[k, s][:], COPY, scale=1.0 / (TAU * N), accum_out=mass[k, s][:])
 
-        def mass_inv(k):
-            inv[k] = work.tile([P, 2], F32, name="inv", tag="inv")
-            nc.vector.reciprocal(inv[k][:], mrow[k][:])
+        def mass_inv(k, s):
+            inv[k, s] = work.tile([P, 1], F32, name="inv")
+            nc.vector.reciprocal(inv[k, s][:], mass[k, s][:])
+
+        grouped = {}
+        codes = {}
+        planes = {}
+
+        def group_tile():
+            return work.tile([P, W, T], BF16, name="grouped", bufs=5, align_bytes=64)
+
+        def interleaved(dst, src):
+            return dst.rearrange("p (c i) t -> p c t i", i=4), src.rearrange("p t (c i) -> p c t i", i=4)
+
+        def gather(k, g):
+            grouped[k, g] = group_tile()
+            dst, src = interleaved(grouped[k, g][:], turned[k, g][:])
+            weights = v_gain[:, g, :].unsqueeze(1).unsqueeze(3).to_broadcast([P, W // 4, T, 4])
+            nc.vector.tensor_tensor(dst, src, weights, MULT)
+
+        def gather_scalar(k, g):
+            scaled = work.tile([P, T, W], BF16, name="scaled")
+            for t in range(T):
+                nc.scalar.activation(scaled[:, t, :], turned[k, g][:, t, :], COPY, scale=v_gain[:, g, t:t + 1])
+            grouped[k, g] = group_tile()
+            dst, src = interleaved(grouped[k, g][:], scaled[:])
+            nc.scalar.copy(dst, src)
+
+        def quant(k, g):
+            codes[k, g] = work.tile([P, W], U32, name="codes", bufs=8, align_bytes=64)
+            planes[k, g] = work.tile([P, W], U8, name="planes", bufs=8, align_bytes=64)
+            nc.vector.quantize_mx(
+                out=codes[k, g][:].bitcast(FP8X4), scales=planes[k, g][:], in_=grouped[k, g][:].rearrange("p r t -> p (r t)")
+            )
 
         proj = {}
 
-        def stage2(i):
-            k, s = divmod(i, 2)
-            cols = slice(P * s, P * (s + 1))
-            for e in range(2):
-                ps = psum.tile([P, KP], F32, name="ps", tag="s")
-                for g in G_ORDER:
-                    nc.tensor.matmul_mx(
-                        out=ps[:],
-                        lhsT=codes[k, g][:, cols].bitcast(FP8X4),
-                        lhsT_scale=planes[k, g][:, cols],
-                        rhs=zs[:, g, 2 * KP * e:2 * KP * (e + 1)].bitcast(FP4X4),
-                        rhs_scale=z_plane[:, g, KP * e:KP * (e + 1)],
-                        start=(g == G_ORDER[0]),
-                        stop=(g == G_ORDER[-1]),
-                    )
-                proj[i, e] = ps
+        def project(k, s, e):
+            proj[k, s, e] = mx_bank("proj")
+            rows = slice(P * s, P * (s + 1))
+            for g in range(GN):
+                nc.tensor.matmul_mx(
+                    out=proj[k, s, e][:],
+                    lhsT=codes[k, g][:, rows].bitcast(FP8X4),
+                    lhsT_scale=planes[k, g][:, rows],
+                    rhs=z_codes[:, g, 2 * KP * e:2 * KP * (e + 1)].bitcast(FP4X4),
+                    rhs_scale=z_plane[:, g, KP * e:KP * (e + 1)],
+                    start=(g == 0),
+                    stop=(g == GN - 1),
+                )
 
-        def finish(i, e):
-            ecols = slice(KP * e, KP * (e + 1))
-            res = work.tile([P, KP], F32, name="res", tag="res", bufs=4)
-            nc.vector.scalar_tensor_tensor(res[:], proj[i, e][:], inv[i // 2][:, i % 2:i % 2 + 1], sq[i][:, ecols], MULT, ADD)
-            nc.sync.dma_start(out=out_view[:, i, ecols], in_=res[:])
+        def finish(k, s, e):
+            cols = slice(KP * e, KP * (e + 1))
+            result = work.tile([P, KP], F32, name="result", bufs=4)
+            nc.vector.scalar_tensor_tensor(result[:], proj[k, s, e][:], inv[k, s][:], quarters[2 * k + s][:, cols], MULT, ADD)
+            nc.sync.dma_start(out=out_view[:, 2 * k + s, cols], in_=result[:])
 
-        turn(3, 0, 0)
-        turn(3, 0, 1)
-        turn_outs(3, 0, "svsv")
-        turn(3, 1, 0)
-        turn(3, 1, 1)
-        turn_outs(3, 1, "svsv")
-        turn(3, 2, 0)
-        turn(3, 2, 1)
-        turn(3, 3, 0)
-        turn(3, 3, 1)
-        turn_outs(3, 2, "svsv")
-        turn_outs(3, 3, "svsv")
-        small = col_scale()
-        for q in range(4):
-            small[q]()
-            quarter(4 + q)
         for g in range(GN):
             weigh(0, g)
-        direct(0, 0)
-        direct(0, 1)
+        gather(0, 0)
+        gather(0, 1)
         quant(0, 0)
-        direct(0, 2)
+        gather(0, 2)
         quant(0, 1)
-        direct(0, 3)
+        gather(0, 3)
         quant(0, 2)
         quant(0, 3)
-        for n in range(1, NP + 1):
-            k = n - 1
-            if k < TURN_FIRST:
-                mass_turn(k)
-            stage2(2 * k)
-            if k >= TURN_FIRST:
-                mass_turn(k)
-            stage2(2 * k + 1)
-            if n in SPLIT:
-                scale(n, 3)
-                interleave(n, 3, "s")
-            if n == NP:
+        for k in range(PAIRS):
+            n = k + 1
+            mass_turn(k, 0)
+            project(k, 0, 0)
+            mass_turn(k, 1)
+            project(k, 0, 1)
+            project(k, 1, 0)
+            project(k, 1, 1)
+            if n == PAIRS:
                 mass_sum(k)
-            if n < NP:
-                for g in range(GN):
-                    if g == SUM_AT:
-                        mass_sum(k)
-                    weigh(n, g)
-                direct(n, 0)
-                direct(n, 1)
-                quant(n, 0)
-                mass_inv(k)
-                finish(2 * k, 0)
-                direct(n, 2)
-                quant(n, 1)
-                finish(2 * k, 1)
-                if n not in SPLIT:
-                    direct(n, 3)
-                quant(n, 2)
-                finish(2 * k + 1, 0)
-                quant(n, 3)
-                finish(2 * k + 1, 1)
-            else:
-                mass_inv(k)
-                for q in range(4):
-                    finish(2 * k + q // 2, q % 2)
+                for s in range(2):
+                    mass_inv(k, s)
+                    for e in range(HALVES):
+                        finish(k, s, e)
+                continue
+            if n in SCALAR_GROUP:
+                gather_scalar(n, 3)
+            weigh(n, 0)
+            weigh(n, 1)
+            mass_sum(k)
+            weigh(n, 2)
+            weigh(n, 3)
+            gather(n, 0)
+            gather(n, 1)
+            quant(n, 0)
+            mass_inv(k, 0)
+            finish(k, 0, 0)
+            gather(n, 2)
+            quant(n, 1)
+            finish(k, 0, 1)
+            if n not in SCALAR_GROUP:
+                gather(n, 3)
+            quant(n, 2)
+            mass_inv(k, 1)
+            finish(k, 1, 0)
+            quant(n, 3)
+            finish(k, 1, 1)

from contextlib import ExitStack

import concourse.mybir as mybir
from concourse.masks import make_identity

M, D, N, E = 1024, 1024, 2048, 1024
EPS = 0.8
TAU = 0.75
FLOPS = 2 * M * D * N + 2 * M * N * E

F32 = mybir.dt.float32
BF16 = mybir.dt.bfloat16
I32 = mybir.dt.int32
U32 = mybir.dt.uint32
U8 = mybir.dt.uint8
FP8X4 = mybir.dt.float8_e4m3fn_x4
FP4X4 = mybir.dt.float4_e2m1fn_x4
ADD = mybir.AluOpType.add
MULT = mybir.AluOpType.mult
MIN = mybir.AluOpType.min
X = mybir.AxisListType.X
EXP = mybir.ActivationFunctionType.Exp
COPY = mybir.ActivationFunctionType.Copy

P = 128
T = 4
KP = P * T
TILES = M // P
XG = D // KP
GN = N // KP
PAIRS = TILES // 2
W = 2 * P
HALVES = E // KP

OUT_EVEN, OUT_ODD = "vsss", "vsvs"
SCALAR_GROUP = (2, 3)


def tile_sinkhorn_step_barycentre_f1_kernel(tc, x, y_words, y_scales, a, b, gain, z_words, z_scales, start, out):
    nc = tc.nc
    with ExitStack() as ctx:
        keep = ctx.enter_context(tc.tile_pool(name="keep", bufs=1))
        work = ctx.enter_context(tc.tile_pool(name="work", bufs=3))
        psum = ctx.enter_context(tc.psum_pool(name="psum", bufs=4))
        ctx.enter_context(tc.manual_schedule())

        def mx_bank(name):
            return psum.tile([P, KP], F32, name=name, tag="mx", bufs=3)

        def turn_bank(shape, name):
            return psum.tile(shape, F32, name=name, tag="turn", bufs=5)

        y_plane = keep.tile([P, XG, N], U8, name="y_plane", align_bytes=64)
        z_plane = keep.tile([P, GN, E], U8, name="z_plane", align_bytes=64)
        warm = keep.tile([P, 1], F32, name="warm")
        ident = keep.tile([P, P], F32, name="ident")
        nc.vector.memset(y_plane[:].rearrange("p g n -> p (g n)").bitcast(I32), 0)
        nc.vector.memset(warm[:], 0.0)
        nc.vector.memset(z_plane[:].rearrange("p g n -> p (g n)").bitcast(I32), 0)
        make_identity(nc, ident[:])
        nc.scalar.activation(warm[:], warm[:], EXP)

        x_view = x.rearrange("(p i) d -> p i d", i=TILES)
        start_view = start.rearrange("(p i) e -> p i e", i=TILES)
        out_view = out.rearrange("(p i) e -> p i e", i=TILES)

        x_rows = [keep.tile([P, D], BF16, name="x_rows%d" % i, align_bytes=64) for i in range(TILES)]
        y_codes = [keep.tile([P, XG, 2 * KP], U8, name="y_codes%d" % g, align_bytes=64) for g in range(GN)]
        z_codes = keep.tile([P, GN, 2 * E], U8, name="z_codes", align_bytes=64)
        starts = [keep.tile([P, E], BF16, name="starts%d" % i) for i in range(TILES)]
        quarters = [keep.tile([P, E], BF16, name="quarters%d" % i) for i in range(TILES)]
        a_sb = keep.tile([P, TILES], BF16, name="a_sb")
        b_sb = keep.tile([P, GN, T], BF16, name="b_sb")
        gain_sb = keep.tile([P, GN, T], BF16, name="gain_sb")

        def load_x(i):
            nc.sync.dma_start(out=x_rows[i][:], in_=x_view[:, i, :])

        def load_y(g):
            cols = slice(2 * KP * g, 2 * KP * (g + 1))
            nc.sync.dma_start(out=y_codes[g][:].bitcast(I32), in_=y_words[:, :, cols].rearrange("g p n -> p g n").bitcast(I32))

        def load_scales(plane, scales):
            for q in range(4):
                rows = scales[:, 4 * q:4 * q + 4, :].rearrange("g r n -> r g n")
                nc.sync.dma_start(out=plane[32 * q:32 * q + 4, :, :].bitcast(I32), in_=rows.bitcast(I32))

        load_x(0)
        load_scales(y_plane, y_scales)
        load_y(0)
        load_y(1)
        load_x(1)
        load_y(2)
        load_y(3)
        load_x(2)
        nc.sync.dma_start(out=a_sb[:], in_=a.rearrange("(p i) -> p i", i=TILES))
        for i in range(3, TILES):
            load_x(i)
        for i in range(TILES):
            nc.sync.dma_start(out=starts[i][:], in_=start_view[:, i, :])
        nc.sync.dma_start(out=b_sb[:], in_=b.rearrange("(g p t) -> p g t", p=P, t=T))
        nc.sync.dma_start(out=gain_sb[:], in_=gain.rearrange("(g p t) -> p g t", p=P, t=T))
        load_scales(z_plane, z_scales)
        nc.sync.dma_start(out=z_codes[:].bitcast(I32), in_=z_words.rearrange("g p n -> p g n").bitcast(I32))

        x_turned = {}
        x_grouped = {}
        x_codes = {}
        x_planes = {}

        def x_turn(i):
            words = x_rows[i][:].bitcast(F32)
            x_turned[i] = turn_bank([P, XG, 2, P], "x_turned")
            for g in range(XG):
                for u in range(2):
                    nc.tensor.transpose(x_turned[i][:, g, u, :], words[:, 2 * P * g + u:2 * P * (g + 1):2], ident[:])

        def x_copy(i):
            x_grouped[i] = work.tile([P, XG, P, T], BF16, name="x_grouped", align_bytes=64)
            dst = x_grouped[i][:].rearrange("p g r t -> p g (r t)").bitcast(F32).rearrange("p g (r u) -> p g r u", u=2)
            nc.scalar.copy(dst, x_turned[i][:].rearrange("p g u r -> p g r u"))

        def x_quant(i):
            x_codes[i] = keep.tile([P, XG, P], U32, name="x_codes%d" % i, align_bytes=64)
            x_planes[i] = keep.tile([P, XG, P], U8, name="x_planes%d" % i, align_bytes=64)
            nc.vector.quantize_mx(
                out=x_codes[i][:].rearrange("p g r -> p (g r)").bitcast(FP8X4),
                scales=x_planes[i][:].rearrange("p g r -> p (g r)"),
                in_=x_grouped[i][:].rearrange("p g r t -> p (g r t)"),
            )

        sums = {}
        kern = {}
        mins = {}
        shift = {}
        row_sum = {}

        def similarity(i, g):
            sums[i, g] = mx_bank("sums")
            for d in range(XG):
                nc.tensor.matmul_mx(
                    out=sums[i, g][:],
                    lhsT=x_codes[i][:, d, :].bitcast(FP8X4),
                    lhsT_scale=x_planes[i][:, d, :],
                    rhs=y_codes[g][:, d, :].bitcast(FP4X4),
                    rhs_scale=y_plane[:, d, KP * g:KP * (g + 1)],
                    start=(d == 0),
                    stop=(d == XG - 1),
                )

        def take_out(i, g):
            if g == 0:
                kern[i] = work.tile([P, GN, T, P], F32, name="kern", tag="kern", bufs=5)
                mins[i] = work.tile([P, GN], F32, name="mins")
            by_slot = sums[i, g][:].rearrange("r (p t) -> r t p", t=T)
            nc.vector.tensor_scalar(kern[i][:, g, :, :], by_slot, -1.0 / EPS, None, MULT, MIN, accum_out=mins[i][:, g:g + 1])

        def row_min(i):
            shift[i] = work.tile([P, 1], F32, name="shift")
            nc.vector.tensor_reduce(shift[i][:], mins[i][:], X, MIN)

        def exponential(i):
            row_sum[i] = work.tile([P, 1], F32, name="row_sum")
            nc.scalar.activation(kern[i][:], kern[i][:], EXP, bias=shift[i][:], scale=-1.0, accum_out=row_sum[i][:])

        a_n = keep.tile([P, TILES], F32, name="a_n")

        def row_scale(i):
            recip = work.tile([P, 1], F32, name="recip")
            nc.vector.reciprocal(recip[:], row_sum[i][:])
            if i + 1 < TILES:
                nc.gpsimd.tensor_scalar(kern[i][:], kern[i][:], recip[:], a_n[:, i:i + 1], MULT, MULT)
            else:
                for g in range(GN):
                    nc.vector.tensor_scalar(kern[i][:, g, :, :], kern[i][:, g, :, :], recip[:], a_n[:, i:i + 1], MULT, MULT)

        def quarter(i, engine):
            engine.tensor_scalar(quarters[i][:], starts[i][:], 1.0 - TAU, 0.0, MULT, ADD)

        turned = {}
        banks = {}
        col_parts = keep.tile([P, GN, T, PAIRS], F32, name="col_parts")

        def turn(k, g):
            for h in range(2):
                banks[k, g, h] = turn_bank([P, 2, 2, P], "banks")
                for t in range(2):
                    for s in range(2):
                        nc.tensor.transpose(banks[k, g, h][:, t, s, :], kern[2 * k + s][:, g, 2 * h + t, :], ident[:])

        def turn_out(k, g, engines):
            turned[k, g] = keep.tile([P, T, W], F32, name="turned%d_%d" % (k, g))
            for t in range(T):
                src = banks[k, g, t // 2][:, t % 2, :, :].rearrange("p s r -> p (s r)")
                part = col_parts[:, g, t, k:k + 1]
                if engines[t] == "v":
                    nc.vector.tensor_scalar(turned[k, g][:, t, :], src, 1.0, None, MULT, ADD, accum_out=part)
                else:
                    nc.scalar.activation(turned[k, g][:, t, :], src, COPY, accum_out=part)

        x_turn(0)
        x_copy(0)
        x_quant(0)
        for i in range(TILES):
            k, half = divmod(i - 3, 2)
            groups = (2 * half, 2 * half + 1) if i >= 3 else ()
            for g in range(GN):
                similarity(i, g)
                if i == 0 and g == 1:
                    x_turn(1)
                    x_copy(1)
            if i + 2 < TILES:
                x_turn(i + 2)
            for g in groups:
                turn(k, g)
            for g in range(GN):
                take_out(i, g)
                if i == 0 and g == 2:
                    x_quant(1)
            row_min(i)
            if i + 2 < TILES:
                x_copy(i + 2)
                x_quant(i + 2)
            if i == 0:
                nc.vector.tensor_scalar(a_n[:], a_sb[:], float(N), None, MULT)
            if i >= 1:
                row_scale(i - 1)
                if 3 <= i <= 6:
                    quarter(i - 3, nc.gpsimd)
            exponential(i)
            for g in groups:
                turn_out(k, g, "vvvv" if i + 1 == TILES else OUT_ODD if g % 2 else OUT_EVEN)

        turn(2, 2)
        turn(2, 3)
        turn_out(2, 2, "ssss")
        turn_out(2, 3, "ssss")
        row_scale(TILES - 1)
        turn(3, 0)
        turn_out(3, 0, "svsv")
        turn(3, 1)
        turn_out(3, 1, "svsv")
        turn(3, 2)
        turn(3, 3)
        turn_out(3, 2, "svsv")
        turn_out(3, 3, "svsv")

        col_sum = keep.tile([P, GN, T], F32, name="col_sum")
        col_recip = keep.tile([P, GN, T], F32, name="col_recip")
        v = keep.tile([P, GN, T], F32, name="v")
        v_gain = keep.tile([P, GN, T], F32, name="v_gain")
        nc.vector.tensor_reduce(col_sum[:], col_parts[:], X, ADD)
        quarter(4, nc.vector)
        nc.vector.reciprocal(col_recip[:], col_sum[:])
        quarter(5, nc.vector)
        nc.vector.scalar_tensor_tensor(v[:], col_recip[:], float(M), b_sb[:], MULT, MULT)
        quarter(6, nc.vector)
        nc.vector.tensor_tensor(v_gain[:], v[:], gain_sb[:], MULT)
        quarter(7, nc.vector)

        plan = {}
        mass_parts = {}
        mass = {}
        inv = {}

        def weigh(k, g):
            if g % 2 == 0:
                plan[k, g // 2] = work.tile([P, 2, T, W], F32, name="plan", tag="kern", bufs=5)
            for t in range(T):
                nc.scalar.activation(plan[k, g // 2][:, g % 2, t, :], turned[k, g][:, t, :], COPY, scale=v[:, g, t:t + 1])

        def mass_turn(k, s):
            mass_parts[k, s] = turn_bank([P, P], "mass_parts")
            for q in range(GN * T):
                g, t = divmod(q, T)
                nc.tensor.matmul(
                    mass_parts[k, s][:],
                    lhsT=plan[k, g // 2][:, g % 2, t, P * s:P * (s + 1)],
                    rhs=ident[:],
                    is_transpose=True,
                    start=(q == 0),
                    stop=(q == GN * T - 1),
                )

        def mass_sum(k):
            for s in range(2):
                mass[k, s] = work.tile([P, 1], F32, name="mass")
                unused = work.tile([P, P], BF16, name="unused")
                nc.scalar.activation(unused[:], mass_parts[k, s][:], COPY, scale=1.0 / (TAU * N), accum_out=mass[k, s][:])

        def mass_inv(k, s):
            inv[k, s] = work.tile([P, 1], F32, name="inv")
            nc.vector.reciprocal(inv[k, s][:], mass[k, s][:])

        grouped = {}
        codes = {}
        planes = {}

        def group_tile():
            return work.tile([P, W, T], BF16, name="grouped", bufs=5, align_bytes=64)

        def interleaved(dst, src):
            return dst.rearrange("p (c i) t -> p c t i", i=4), src.rearrange("p t (c i) -> p c t i", i=4)

        def gather(k, g):
            grouped[k, g] = group_tile()
            dst, src = interleaved(grouped[k, g][:], turned[k, g][:])
            weights = v_gain[:, g, :].unsqueeze(1).unsqueeze(3).to_broadcast([P, W // 4, T, 4])
            nc.vector.tensor_tensor(dst, src, weights, MULT)

        def gather_scalar(k, g):
            scaled = work.tile([P, T, W], BF16, name="scaled")
            for t in range(T):
                nc.scalar.activation(scaled[:, t, :], turned[k, g][:, t, :], COPY, scale=v_gain[:, g, t:t + 1])
            grouped[k, g] = group_tile()
            dst, src = interleaved(grouped[k, g][:], scaled[:])
            nc.scalar.copy(dst, src)

        def quant(k, g):
            codes[k, g] = work.tile([P, W], U32, name="codes", bufs=8, align_bytes=64)
            planes[k, g] = work.tile([P, W], U8, name="planes", bufs=8, align_bytes=64)
            nc.vector.quantize_mx(
                out=codes[k, g][:].bitcast(FP8X4), scales=planes[k, g][:], in_=grouped[k, g][:].rearrange("p r t -> p (r t)")
            )

        proj = {}

        def project(k, s, e):
            proj[k, s, e] = mx_bank("proj")
            rows = slice(P * s, P * (s + 1))
            for g in range(GN):
                nc.tensor.matmul_mx(
                    out=proj[k, s, e][:],
                    lhsT=codes[k, g][:, rows].bitcast(FP8X4),
                    lhsT_scale=planes[k, g][:, rows],
                    rhs=z_codes[:, g, 2 * KP * e:2 * KP * (e + 1)].bitcast(FP4X4),
                    rhs_scale=z_plane[:, g, KP * e:KP * (e + 1)],
                    start=(g == 0),
                    stop=(g == GN - 1),
                )

        def finish(k, s, e):
            cols = slice(KP * e, KP * (e + 1))
            result = work.tile([P, KP], F32, name="result", bufs=4)
            nc.vector.scalar_tensor_tensor(result[:], proj[k, s, e][:], inv[k, s][:], quarters[2 * k + s][:, cols], MULT, ADD)
            nc.sync.dma_start(out=out_view[:, 2 * k + s, cols], in_=result[:])

        for g in range(GN):
            weigh(0, g)
        gather(0, 0)
        gather(0, 1)
        quant(0, 0)
        gather(0, 2)
        quant(0, 1)
        gather(0, 3)
        quant(0, 2)
        quant(0, 3)
        for k in range(PAIRS):
            n = k + 1
            mass_turn(k, 0)
            project(k, 0, 0)
            mass_turn(k, 1)
            project(k, 0, 1)
            project(k, 1, 0)
            project(k, 1, 1)
            if n == PAIRS:
                mass_sum(k)
                for s in range(2):
                    mass_inv(k, s)
                    for e in range(HALVES):
                        finish(k, s, e)
                continue
            if n in SCALAR_GROUP:
                gather_scalar(n, 3)
            weigh(n, 0)
            weigh(n, 1)
            mass_sum(k)
            weigh(n, 2)
            weigh(n, 3)
            gather(n, 0)
            gather(n, 1)
            quant(n, 0)
            mass_inv(k, 0)
            finish(k, 0, 0)
            gather(n, 2)
            quant(n, 1)
            finish(k, 0, 1)
            if n not in SCALAR_GROUP:
                gather(n, 3)
            quant(n, 2)
            mass_inv(k, 1)
            finish(k, 1, 0)
            quant(n, 3)
            finish(k, 1, 1)
